import numpy as np
import ml_dtypes


def mxq(x, axis, fmt="e4m3"):
    dtype, down = {"e4m3": (ml_dtypes.float8_e4m3fn, 7), "e5m2": (ml_dtypes.float8_e5m2, 14)}[fmt]
    v = np.moveaxis(np.asarray(x, np.float32).astype(ml_dtypes.bfloat16).astype(np.float64), axis, -1)
    blocks = v.reshape(v.shape[:-1] + (-1, 32))
    amax = np.abs(blocks).max(-1, keepdims=True)
    byte = np.maximum(np.where(amax > 0, np.frexp(amax)[1] - 1 + 127, 0) - down, 1)
    scale = np.exp2(byte - 127.0)
    codes = (blocks / scale).astype(np.float32).astype(dtype).astype(np.float64)
    return np.moveaxis((codes * scale).reshape(v.shape), -1, axis)


WIDE = False


def mx_kscale(k):
    if not WIDE:
        return np.ones(k)
    levels = np.array([24, -24, 12, -12, 0])
    if k % 512:
        return np.exp2(np.random.permutation(np.resize(levels, k // 32))).repeat(32)
    a = np.empty((k // 512, 16))
    for p in range(k // 512):
        a[p, :8] = np.random.permutation(np.resize(levels, 8))
        for g in range(8):
            far = levels[np.abs(levels - a[p, g]) >= 10]
            a[p, g + 8] = far[np.random.randint(len(far))]
    return np.exp2(a.ravel()).repeat(32)


def f64(x):
    return np.asarray(x).astype(np.float64)


def striped(idx):
    return np.tile(idx.reshape(-1, 16).T, (8, 1)).astype(np.uint16)


def unstriped(offs):
    return offs[:16].T.reshape(-1).astype(np.int64)


E2M1 = np.array([0.0, 0.5, 1.0, 1.5, 2.0, 3.0, 4.0, 6.0, -0.0, -0.5, -1.0, -1.5, -2.0, -3.0, -4.0, -6.0])


def pack_weight(w, fmt):
    k, n = w.shape
    w = f64(np.asarray(w, np.float32).astype(ml_dtypes.bfloat16)).reshape(k // 32, 32, n)
    amax = np.abs(w).max(1)
    if fmt == "e4m3":
        byte = np.frexp(amax)[1] - 1 + 127 - 7
    else:
        mant, ex = np.frexp(amax / 6.0)
        byte = np.where(mant > 0.5, ex, ex - 1) + 127
    byte = np.clip(np.where(amax > 0, byte, 1), 1, 254)
    scaled = (w * np.exp2(127.0 - byte)[:, None, :]).reshape(k, n).astype(np.float32)
    by_word = np.ascontiguousarray(scaled.reshape(k // 512, 128, 4, n).transpose(0, 1, 3, 2))
    if fmt == "e4m3":
        words = by_word.astype(ml_dtypes.float8_e4m3fn).view(np.uint8)
    else:
        c = by_word.astype(ml_dtypes.float4_e2m1fn).view(np.uint8) & 0xF
        words = (c[..., 0::2] | (c[..., 1::2] << 4)).reshape(k // 512, 128, 2 * n)
    return np.ascontiguousarray(words), np.ascontiguousarray(byte.astype(np.uint8).reshape(k // 512, 16, n))


def unpack_weight(words, scales, fmt):
    g, _, n = scales.shape
    words = np.ascontiguousarray(words).reshape(g, 128, n, -1)
    if fmt == "e4m3":
        vals = words.view(ml_dtypes.float8_e4m3fn).astype(np.float64)
    else:
        nib = np.empty((g, 128, n, 4), np.uint8)
        nib[..., 0::2] = words & 0xF
        nib[..., 1::2] = words >> 4
        vals = E2M1[nib]
    vals = vals * np.repeat(np.exp2(scales.astype(np.float64) - 127.0), 8, axis=1)[..., None]
    return vals.transpose(0, 1, 3, 2).reshape(g * 512, n)


def pack_table4(v):
    words, scales = pack_weight(v, "e2m1")
    g, t = words.shape[0] // 2, v.shape[1]
    return np.ascontiguousarray(words.reshape(g, 2, 128, t, 2).transpose(0, 2, 3, 1, 4).reshape(g, 128, t, 4)), scales


def unpack_table4(words, scales):
    g, _, t, _ = words.shape
    return unpack_weight(words.reshape(g, 128, t, 2, 2).transpose(0, 3, 1, 2, 4).reshape(2 * g, 128, 2 * t), scales, "e2m1")


K, M, N, J, T = 1024, 1024, 512, 1024, 2048


def setup_inputs():
    n = np.random.standard_normal
    s = mx_kscale(K)[:, None]
    u = mx_kscale(J)[:, None]
    al = n((J, N)) / np.sqrt(J) / u
    p_tab = pack_table4(0.5 * n((K, T)) / np.sqrt(K) / s)
    p_al8 = pack_weight(al[:512], "e4m3")
    p_al4 = pack_weight(al[512:], "e2m1")
    return {
        "x": (n((K, M)) * s).astype(np.float32),
        "tab_words": p_tab[0],
        "tab_scales": p_tab[1],
        "cw": (np.random.uniform(0.5, 2.0, J) * u[:, 0]).astype(np.float32),
        "cb": (0.3 * n(J)).astype(np.float32),
        "al8_words": p_al8[0],
        "al8_scales": p_al8[1],
        "al4_words": p_al4[0],
        "al4_scales": p_al4[1],
        "offs": striped(np.random.permutation(T)[:J]),
    }


def reference(x, tab_words, tab_scales, cw, cb, al8_words, al8_scales, al4_words, al4_scales, offs):
    idx = unstriped(offs)
    x_ = mxq(f64(x), 0, "e4m3")
    tab_ = unpack_table4(tab_words, tab_scales)[:, idx]
    d = tab_.T @ x_
    h = f64(cw)[:, None] * np.tanh(d + f64(cb)[:, None])
    h_ = mxq(h, 0, "e4m3")
    al8_ = unpack_weight(al8_words, al8_scales, "e4m3")
    al4_ = unpack_weight(al4_words, al4_scales, "e2m1")
    y = al8_.T @ h_[:512] + al4_.T @ h_[512:]
    return y

@@ -1,0 +1,284 @@
+from contextlib import ExitStack
+
+import concourse.mybir as mybir
+
+K, M, N, J, T = 1024, 1024, 512, 1024, 2048
+FLOPS = 2 * K * J * M + 2 * J * N * M
+
+F32 = mybir.dt.float32
+BF16 = mybir.dt.bfloat16
+I32 = mybir.dt.int32
+U32 = mybir.dt.uint32
+U16 = mybir.dt.uint16
+U8 = mybir.dt.uint8
+FP8X4 = mybir.dt.float8_e4m3fn_x4
+FP4X4 = mybir.dt.float4_e2m1fn_x4
+TANH = mybir.ActivationFunctionType.Tanh
+MULT = mybir.AluOpType.mult
+
+P = 128
+PACK = 4
+K_PASS = P * PACK
+HALF = 512
+PIECE = 256
+RUN = 4
+NARROW = 128
+VECTOR_CASTS = {(1,1),(0,2),(0,3),(1,3)}
+WARM_PASSES = 0
+AFTER = {"picked_words1":"x_raw10","h_grouped1_0":"x_raw13","h_grouped0_256":"x_grouped02","tanh01":"x_raw12"}
+
+
+def tile_list_kernl_tanh_mix_none_kernel(
+    tc, x, tab_words, tab_scales, cw, cb, al8_words, al8_scales, al4_words, al4_scales, offs, out
+):
+    nc = tc.nc
+    with ExitStack() as ctx:
+        keep = ctx.enter_context(tc.tile_pool(name="keep", bufs=1))
+        share = ctx.enter_context(tc.tile_pool(name="share", bufs=1))
+        psum = ctx.enter_context(tc.psum_pool(name="psum", bufs=4))
+
+        def sbuf(shape, dtype, name):
+            return share.tile(shape, dtype, name=name, tag=AFTER.get(name, name), align_bytes=64)
+
+        offsets = keep.tile([P, J // 16], U16, name="offsets")
+        nc.sync.dma_start(offsets[:], offs)
+
+        scale_window = sbuf([P, T // 4], I32, "scale_window")
+        nc.vector.memset(scale_window[:], 0)
+        warm_in = sbuf([P, 1], F32, "warm_in")
+        nc.vector.memset(warm_in[:], 0.0)
+        warm_out = sbuf([P, 1], F32, "warm_out")
+        nc.scalar.activation(out=warm_out[:], in_=warm_in[:], func=TANH)
+        shifted = sbuf([P, 2, K_PASS // 4], I32, "shifted")
+        nc.vector.memset(shifted[:], 0)
+        al_planes = sbuf([P, 2, N // 4], I32, "al_planes")
+        nc.vector.memset(al_planes[:], 0)
+
+        cb_sb = sbuf([P, 2, PACK], F32, "cb_sb")
+        nc.sync.dma_start(cb_sb[:], cb.rearrange("(g p t) -> p g t", g=2, t=PACK))
+        scale_rows = tab_scales.bitcast(I32).rearrange("a (q r) w -> r q a w", r=4)
+        for r in range(4):
+            nc.sync.dma_start(scale_window[r:P:16, :], scale_rows[r])
+
+        x_raw = {}
+
+        def load_x(a, c):
+            raw = sbuf([P, PACK, PIECE], F32, f"x_raw{a}{c}")
+            rows = x[a * K_PASS : (a + 1) * K_PASS, c * PIECE : (c + 1) * PIECE]
+            nc.sync.dma_start(raw[:], rows.rearrange("(p i) w -> p i w", i=PACK))
+            x_raw[a, c] = raw
+
+        load_x(0, 0)
+        word_window = sbuf([P, T], I32, "word_window")
+        nc.sync.dma_start(word_window[:], tab_words[0].rearrange("p t b -> p (t b)").bitcast(I32))
+        load_x(1, 0)
+        load_x(0, 1)
+        cw_sb = sbuf([P, 2, PACK], F32, "cw_sb")
+        nc.sync.dma_start(cw_sb[:], cw.rearrange("(g p t) -> p g t", g=2, t=PACK))
+        load_x(1, 1)
+        for c in (2, 3):
+            load_x(0, c)
+            load_x(1, c)
+        al8_sb = sbuf([P, N], I32, "al8_sb")
+        nc.sync.dma_start(al8_sb[:], al8_words[0].rearrange("p n b -> p (n b)").bitcast(I32))
+        al4_sb = sbuf([P, N // 2], I32, "al4_sb")
+        nc.sync.dma_start(al4_sb[:], al4_words[0].bitcast(I32))
+        for g, scales in enumerate((al8_scales, al4_scales)):
+            for q in range(4):
+                nc.sync.dma_start(al_planes[32 * q : 32 * q + 4, g, :], scales[0, 4 * q : 4 * q + 4, :].bitcast(I32))
+
+        tab_planes = {}
+
+        def pick_scales(g):
+            picked = sbuf([P, K_PASS], U8, f"picked_scales{g}")
+            nc.vector.tensor_copy(picked[:], scale_window[:].bitcast(U8).indirect(offsets[:, 32 * g : 32 * g + 32]))
+            plane = sbuf([P, K_PASS // 4], I32, f"tab_plane{g}")
+            nc.vector.tensor_copy(
+                plane[:].bitcast(U8).rearrange("p (t c) -> p t c", t=PACK),
+                picked[:].rearrange("p (c t) -> p t c", t=PACK),
+            )
+            nc.gpsimd.dma_start(shifted[0:112, g, :], plane[16:P, :])
+            tab_planes[g, 0] = plane[:].bitcast(U8)
+            tab_planes[g, 1] = shifted[:, g, :].bitcast(U8)
+
+        tab_codes = {}
+
+        def pick_words(g):
+            codes = sbuf([P, 2, K_PASS], U16, f"tab_codes{g}")
+            picked = sbuf([P, 2, K_PASS // 2], U32, f"picked_words{g}")
+            for h in range(2):
+                nc.vector.tensor_copy(
+                    picked[:, h, :].rearrange("p (t c) -> p c t", t=PACK),
+                    word_window[:].bitcast(U32).indirect(offsets[:, 32 * g + 16 * h : 32 * g + 16 * h + 16]),
+                )
+            for h in range(2):
+                nc.vector.tensor_copy(
+                    codes[:].rearrange("p a (t c) -> p a t c", t=PACK)[:, :, :, 64 * h : 64 * h + 64],
+                    picked[:, h, :].bitcast(U16).rearrange("p (t c a) -> p a t c", t=PACK, a=2),
+                )
+            tab_codes[g] = codes
+
+        x_codes, x_scales, x_grouped = {}, {}, {}
+
+        def round_x(a, c):
+            half = c // 2
+            key = (a, c) if half == 0 else (a, 2)
+            if key not in x_grouped:
+                width = PIECE if half == 0 else HALF
+                x_grouped[key] = sbuf([P, width * PACK], BF16, f"x_grouped{key[0]}{key[1]}")
+            lo = 0 if half == 0 else (c - 2) * PIECE * PACK
+            dst = x_grouped[key][:, lo : lo + PIECE * PACK].rearrange("p (c i t) -> p c t i", i=RUN, t=PACK)
+            src = x_raw[a, c][:].rearrange("p t (c i) -> p c t i", i=RUN)
+            if (a, c) in VECTOR_CASTS:
+                nc.vector.tensor_copy(dst, src)
+            else:
+                nc.scalar.copy(dst, src)
+
+        def quantize_x(a, c):
+            width = PIECE if c < 2 else HALF
+            x_codes[a, c] = sbuf([P, width], U32, f"x_codes{a}{c}")
+            x_scales[a, c] = sbuf([P, width], U8, f"x_scales{a}{c}")
+            nc.vector.quantize_mx(out=x_codes[a, c][:].bitcast(FP8X4), scales=x_scales[a, c][:], in_=x_grouped[a, c][:])
+
+        def table_pass(dst, g, t, a, c, cols, start, stop):
+            nc.tensor.matmul_mx(
+                out=dst,
+                lhsT=tab_codes[g][:, a, t * P : (t + 1) * P].bitcast(FP4X4),
+                lhsT_scale=tab_planes[g, a][:, t * P : (t + 1) * P],
+                rhs=x_codes[a, c][:, cols].bitcast(FP8X4),
+                rhs_scale=x_scales[a, c][:, cols],
+                start=start,
+                stop=stop,
+            )
+
+        tanh_out = {}
+
+        def kernel_values(g, c, n_cols, piece):
+            width = PIECE if c < 2 else HALF
+            th = sbuf([P, PACK, width], F32, f"tanh{g}{c}")
+            banks = []
+            for t in range(PACK):
+                d = psum.tile([P, HALF], F32, name="d")
+                for lo in range(0, width, n_cols):
+                    for a in range(2):
+                        table_pass(d[:, lo : lo + n_cols], g, t, a, c, slice(lo, lo + n_cols), a == 0, a == 1)
+                banks.append(d)
+            for lo in range(0, width, piece):
+                for t in range(PACK):
+                    nc.scalar.activation(
+                        out=th[:, t, lo : lo + piece], in_=banks[t][:, lo : lo + piece], func=TANH, bias=cb_sb[:, g, t : t + 1]
+                    )
+            tanh_out[g, c] = th
+
+        h_codes = [sbuf([P, M], U32, f"h_codes{g}") for g in range(2)]
+        h_scales = [sbuf([P, M], U8, f"h_scales{g}") for g in range(2)]
+        h_grouped = {}
+
+        def weigh_h(g, m0, width):
+            c = min(m0 // PIECE, 2)
+            lo = m0 - c * PIECE
+            grouped = sbuf([P, width * PACK], BF16, f"h_grouped{g}_{m0}")
+            nc.vector.tensor_tensor(
+                grouped[:].rearrange("p (c i t) -> p c t i", i=RUN, t=PACK),
+                tanh_out[g, c][:, :, lo : lo + width].rearrange("p t (c i) -> p c t i", i=RUN),
+                cw_sb[:, g, :].rearrange("p (c t i) -> p c t i", c=1, i=1).to_broadcast([P, width // RUN, PACK, RUN]),
+                MULT,
+            )
+            h_grouped[g, m0] = grouped
+
+        def quantize_h(g, m0, width):
+            cols = slice(m0, m0 + width)
+            nc.vector.quantize_mx(
+                out=h_codes[g][:, cols].bitcast(FP8X4), scales=h_scales[g][:, cols], in_=h_grouped[g, m0][:]
+            )
+
+        def output_pass(dst, n, g, cols):
+            if g == 0:
+                weights = al8_sb[:, n * P : (n + 1) * P].bitcast(FP8X4)
+            else:
+                weights = al4_sb[:, n * P // 2 : (n + 1) * P // 2].bitcast(FP4X4)
+            nc.tensor.matmul_mx(
+                out=dst,
+                lhsT=weights,
+                lhsT_scale=al_planes[:, g, :].bitcast(U8)[:, n * P : (n + 1) * P],
+                rhs=h_codes[g][:, cols].bitcast(FP8X4),
+                rhs_scale=h_scales[g][:, cols],
+                start=(g == 0),
+                stop=(g == 1),
+            )
+
+        def copy_out(engine, dst, src):
+            if engine == "v":
+                nc.vector.tensor_copy(dst, src)
+            else:
+                nc.scalar.copy(dst, src)
+
+        def output_wide(m0):
+            cols = slice(m0, m0 + HALF)
+            for n in range(N // P):
+                y = psum.tile([P, HALF], F32, name="y")
+                for g in range(2):
+                    output_pass(y[:], n, g, cols)
+                staged = sbuf([P, HALF], F32, f"y_wide{n}")
+                copy_out("s", staged[:], y[:])
+                nc.sync.dma_start(out[n * P : (n + 1) * P, cols], staged[:])
+
+        def output_narrow(m0, n0, count, engine):
+            cols = slice(m0, m0 + NARROW)
+            y = psum.tile([P, HALF], F32, name="y")
+            for i in range(count):
+                for g in range(2):
+                    output_pass(y[:, i * NARROW : (i + 1) * NARROW], n0 + i, g, cols)
+            staged = sbuf([P, count, NARROW], F32, f"y_narrow{m0}_{n0}")
+            copy_out(engine, staged[:].rearrange("p n m -> p (n m)"), y[:, : count * NARROW])
+            nc.sync.dma_start(
+                out[n0 * P : (n0 + count) * P, cols].rearrange("(n p) m -> p n m", p=P), staged[:]
+            )
+
+        pick_scales(0)
+        pick_scales(1)
+        round_x(0, 0)
+        quantize_x(0, 0)
+        pick_words(0)
+        round_x(1, 0)
+        quantize_x(1, 0)
+        for w in range(WARM_PASSES):
+            warm = psum.tile([P, HALF], F32, name="y")
+            table_pass(warm[:, :PIECE], 0, w % PACK, 0, 0, slice(0, PIECE), True, True)
+        round_x(0, 1)
+        kernel_values(0, 0, NARROW, PIECE)
+        pick_words(1)
+        round_x(1, 1)
+        quantize_x(0, 1)
+        quantize_x(1, 1)
+        for c in (2, 3):
+            for a in range(2):
+                round_x(a, c)
+        quantize_x(0, 2)
+        quantize_x(1, 2)
+        kernel_values(1, 0, NARROW, PIECE)
+        kernel_values(0, 1, NARROW, PIECE)
+        kernel_values(1, 1, NARROW, PIECE)
+        kernel_values(0, 2, HALF, HALF)
+        kernel_values(1, 2, HALF, PIECE)
+        weigh_h(0, 0, PIECE)
+        weigh_h(1, 0, PIECE)
+        quantize_h(0, 0, PIECE)
+        weigh_h(0, PIECE, PIECE)
+        quantize_h(1, 0, PIECE)
+        weigh_h(1, PIECE, PIECE)
+        quantize_h(0, PIECE, PIECE)
+        quantize_h(1, PIECE, PIECE)
+        output_wide(0)
+        weigh_h(0, HALF, HALF)
+        weigh_h(1, HALF, NARROW)
+        quantize_h(0, HALF, HALF)
+        for m0 in range(HALF, M, NARROW):
+            if m0 + NARROW < M:
+                weigh_h(1, m0 + NARROW, NARROW)
+            quantize_h(1, m0, NARROW)
+            if m0 + NARROW < M:
+                output_narrow(m0, 0, 4, "s")
+            else:
+                output_narrow(m0, 0, 2, "s")
+                output_narrow(m0, 2, 2, "v")

@@ -21,11 +21,11 @@ PACK = 4
 K_PASS = P * PACK
 HALF = 512
 PIECE = 256
-RUN = 4
+RUN = 2
 NARROW = 128
-VECTOR_CASTS = {(1,1),(0,2),(0,3),(1,3)}
+VECTOR_CASTS = {(1,1),(0,2),(1,2),(1,3)}
 WARM_PASSES = 0
-AFTER = {"picked_words1":"x_raw10","h_grouped1_0":"x_raw13","h_grouped0_256":"x_grouped02","tanh01":"x_raw12"}
+AFTER = {"picked_words1":"x_raw10","tab_plane":"x_raw00","tanh01":"x_raw02","h_grouped1_0":"x_raw12","h_grouped0_256":"x_grouped12","h_grouped1_256":"x_grouped02"}
 
 
 def tile_list_kernl_tanh_mix_none_kernel(
@@ -76,9 +76,11 @@ def tile_list_kernl_tanh_mix_none_kernel(
         cw_sb = sbuf([P, 2, PACK], F32, "cw_sb")
         nc.sync.dma_start(cw_sb[:], cw.rearrange("(g p t) -> p g t", g=2, t=PACK))
         load_x(1, 1)
-        for c in (2, 3):
-            load_x(0, c)
-            load_x(1, c)
+        for a in range(2):
+            raw = sbuf([P, PACK, HALF], F32, f"x_raw{a}2")
+            rows = x[a * K_PASS : (a + 1) * K_PASS, HALF:]
+            nc.sync.dma_start(raw[:], rows.rearrange("(p i) w -> p i w", i=PACK))
+            x_raw[a, 2], x_raw[a, 3] = raw[:, :, :PIECE], raw[:, :, PIECE:]
         al8_sb = sbuf([P, N], I32, "al8_sb")
         nc.sync.dma_start(al8_sb[:], al8_words[0].rearrange("p n b -> p (n b)").bitcast(I32))
         al4_sb = sbuf([P, N // 2], I32, "al4_sb")
@@ -88,17 +90,16 @@ def tile_list_kernl_tanh_mix_none_kernel(
                 nc.sync.dma_start(al_planes[32 * q : 32 * q + 4, g, :], scales[0, 4 * q : 4 * q + 4, :].bitcast(I32))
 
         tab_planes = {}
+        plane = sbuf([P, 2, K_PASS // 4], I32, "tab_plane")
 
         def pick_scales(g):
             picked = sbuf([P, K_PASS], U8, f"picked_scales{g}")
             nc.vector.tensor_copy(picked[:], scale_window[:].bitcast(U8).indirect(offsets[:, 32 * g : 32 * g + 32]))
-            plane = sbuf([P, K_PASS // 4], I32, f"tab_plane{g}")
             nc.vector.tensor_copy(
-                plane[:].bitcast(U8).rearrange("p (t c) -> p t c", t=PACK),
+                plane[:, g, :].bitcast(U8).rearrange("p (t c) -> p t c", t=PACK),
                 picked[:].rearrange("p (c t) -> p t c", t=PACK),
             )
-            nc.gpsimd.dma_start(shifted[0:112, g, :], plane[16:P, :])
-            tab_planes[g, 0] = plane[:].bitcast(U8)
+            tab_planes[g, 0] = plane[:, g, :].bitcast(U8)
             tab_planes[g, 1] = shifted[:, g, :].bitcast(U8)
 
         tab_codes = {}
@@ -128,7 +129,7 @@ def tile_list_kernl_tanh_mix_none_kernel(
                 x_grouped[key] = sbuf([P, width * PACK], BF16, f"x_grouped{key[0]}{key[1]}")
             lo = 0 if half == 0 else (c - 2) * PIECE * PACK
             dst = x_grouped[key][:, lo : lo + PIECE * PACK].rearrange("p (c i t) -> p c t i", i=RUN, t=PACK)
-            src = x_raw[a, c][:].rearrange("p t (c i) -> p c t i", i=RUN)
+            src = x_raw[a, c][:, :, :].rearrange("p t (c i) -> p c t i", i=RUN)
             if (a, c) in VECTOR_CASTS:
                 nc.vector.tensor_copy(dst, src)
             else:
@@ -223,20 +224,22 @@ def tile_list_kernl_tanh_mix_none_kernel(
                 copy_out("s", staged[:], y[:])
                 nc.sync.dma_start(out[n * P : (n + 1) * P, cols], staged[:])
 
-        def output_narrow(m0, n0, count, engine):
-            cols = slice(m0, m0 + NARROW)
+        def output_narrow(m0, width, n0, count, engine):
             y = psum.tile([P, HALF], F32, name="y")
             for i in range(count):
-                for g in range(2):
-                    output_pass(y[:, i * NARROW : (i + 1) * NARROW], n0 + i, g, cols)
-            staged = sbuf([P, count, NARROW], F32, f"y_narrow{m0}_{n0}")
-            copy_out(engine, staged[:].rearrange("p n m -> p (n m)"), y[:, : count * NARROW])
+                for lo in range(0, width, NARROW):
+                    for g in range(2):
+                        dst = y[:, i * width + lo : i * width + lo + NARROW]
+                        output_pass(dst, n0 + i, g, slice(m0 + lo, m0 + lo + NARROW))
+            staged = sbuf([P, count, width], F32, f"y_narrow{m0}_{n0}")
+            copy_out(engine, staged[:].rearrange("p n m -> p (n m)"), y[:, : count * width])
             nc.sync.dma_start(
-                out[n0 * P : (n0 + count) * P, cols].rearrange("(n p) m -> p n m", p=P), staged[:]
+                out[n0 * P : (n0 + count) * P, m0 : m0 + width].rearrange("(n p) m -> p n m", p=P), staged[:]
             )
 
         pick_scales(0)
         pick_scales(1)
+        nc.scalar.dma_start(shifted[0:112], plane[16:P])
         round_x(0, 0)
         quantize_x(0, 0)
         pick_words(0)
@@ -270,15 +273,18 @@ def tile_list_kernl_tanh_mix_none_kernel(
         quantize_h(0, PIECE, PIECE)
         quantize_h(1, PIECE, PIECE)
         output_wide(0)
-        weigh_h(0, HALF, HALF)
-        weigh_h(1, HALF, NARROW)
-        quantize_h(0, HALF, HALF)
-        for m0 in range(HALF, M, NARROW):
-            if m0 + NARROW < M:
-                weigh_h(1, m0 + NARROW, NARROW)
-            quantize_h(1, m0, NARROW)
-            if m0 + NARROW < M:
-                output_narrow(m0, 0, 4, "s")
-            else:
-                output_narrow(m0, 0, 2, "s")
-                output_narrow(m0, 2, 2, "v")
+        weigh_h(0, 512, 256)
+        weigh_h(1, 512, 256)
+        quantize_h(0, 512, 256)
+        weigh_h(0, 768, 256)
+        quantize_h(1, 512, 256)
+        output_narrow(512, 256, 0, 2, "s")
+        output_narrow(512, 256, 2, 2, "s")
+        weigh_h(1, 768, 128)
+        quantize_h(0, 768, 256)
+        weigh_h(1, 896, 128)
+        quantize_h(1, 768, 128)
+        output_narrow(768, 128, 0, 4, "s")
+        quantize_h(1, 896, 128)
+        output_narrow(896, 128, 0, 2, "v")
+        output_narrow(896, 128, 2, 2, "s")

@@ -23,9 +23,11 @@ HALF = 512
 PIECE = 256
 RUN = 2
 NARROW = 128
-VECTOR_CASTS = {(1,1),(0,2),(1,2),(1,3)}
-WARM_PASSES = 0
-AFTER = {"picked_words1":"x_raw10","tab_plane":"x_raw00","tanh01":"x_raw02","h_grouped1_0":"x_raw12","h_grouped0_256":"x_grouped12","h_grouped1_256":"x_grouped02"}
+VECTOR_CASTS = {(1, 1), (1, 2), (0, 3), (1, 3)}
+WARM_PASSES = 4
+WIDTH = {0: 256, 1: 256, 2: 256, 3: 256}
+FIRST = (0, 1, 2, 3)
+AFTER = {"picked_words10":"picked_words00","picked_words11":"x_raw10","h_grouped1_896":"h_grouped0_768"}
 
 
 def tile_list_kernl_tanh_mix_none_kernel(
@@ -52,7 +54,7 @@ def tile_list_kernl_tanh_mix_none_kernel(
         shifted = sbuf([P, 2, K_PASS // 4], I32, "shifted")
         nc.vector.memset(shifted[:], 0)
         al_planes = sbuf([P, 2, N // 4], I32, "al_planes")
-        nc.vector.memset(al_planes[:], 0)
+        nc.gpsimd.memset(al_planes[:], 0)
 
         cb_sb = sbuf([P, 2, PACK], F32, "cb_sb")
         nc.sync.dma_start(cb_sb[:], cb.rearrange("(g p t) -> p g t", g=2, t=PACK))
@@ -60,34 +62,37 @@ def tile_list_kernl_tanh_mix_none_kernel(
         for r in range(4):
             nc.sync.dma_start(scale_window[r:P:16, :], scale_rows[r])
 
-        x_raw = {}
-
-        def load_x(a, c):
-            raw = sbuf([P, PACK, PIECE], F32, f"x_raw{a}{c}")
-            rows = x[a * K_PASS : (a + 1) * K_PASS, c * PIECE : (c + 1) * PIECE]
-            nc.sync.dma_start(raw[:], rows.rearrange("(p i) w -> p i w", i=PACK))
-            x_raw[a, c] = raw
-
-        load_x(0, 0)
-        word_window = sbuf([P, T], I32, "word_window")
-        nc.sync.dma_start(word_window[:], tab_words[0].rearrange("p t b -> p (t b)").bitcast(I32))
-        load_x(1, 0)
-        load_x(0, 1)
-        cw_sb = sbuf([P, 2, PACK], F32, "cw_sb")
-        nc.sync.dma_start(cw_sb[:], cw.rearrange("(g p t) -> p g t", g=2, t=PACK))
-        load_x(1, 1)
-        for a in range(2):
-            raw = sbuf([P, PACK, HALF], F32, f"x_raw{a}2")
-            rows = x[a * K_PASS : (a + 1) * K_PASS, HALF:]
-            nc.sync.dma_start(raw[:], rows.rearrange("(p i) w -> p i w", i=PACK))
-            x_raw[a, 2], x_raw[a, 3] = raw[:, :, :PIECE], raw[:, :, PIECE:]
-        al8_sb = sbuf([P, N], I32, "al8_sb")
-        nc.sync.dma_start(al8_sb[:], al8_words[0].rearrange("p n b -> p (n b)").bitcast(I32))
-        al4_sb = sbuf([P, N // 2], I32, "al4_sb")
-        nc.sync.dma_start(al4_sb[:], al4_words[0].bitcast(I32))
         for g, scales in enumerate((al8_scales, al4_scales)):
             for q in range(4):
-                nc.sync.dma_start(al_planes[32 * q : 32 * q + 4, g, :], scales[0, 4 * q : 4 * q + 4, :].bitcast(I32))
+                nc.gpsimd.dma_start(al_planes[32 * q : 32 * q + 4, g, :], scales[0, 4 * q : 4 * q + 4, :].bitcast(I32))
+
+        x_raw = {}
+
+        def load_x(a, c0, count=1):
+            raw = sbuf([P, PACK, count * PIECE], F32, f"x_raw{a}{c0}")
+            rows = x[a * K_PASS : (a + 1) * K_PASS, c0 * PIECE : (c0 + count) * PIECE]
+            nc.sync.dma_start(raw[:], rows.rearrange("(p i) w -> p i w", i=PACK))
+            for c in range(count):
+                x_raw[a, c0 + c] = raw[:, :, c * PIECE : (c + 1) * PIECE]
+
+        word_window = sbuf([P, T], I32, "word_window")
+
+        def load_words():
+            nc.sync.dma_start(word_window[:], tab_words[0].rearrange("p t b -> p (t b)").bitcast(I32))
+
+        cw_sb = sbuf([P, 2, PACK], F32, "cw_sb")
+        al8_sb = sbuf([P, N], I32, "al8_sb")
+        al4_sb = sbuf([P, N // 2], I32, "al4_sb")
+
+        def load_cw():
+            nc.gpsimd.dma_start(cw_sb[:], cw.rearrange("(g p t) -> p g t", g=2, t=PACK))
+
+        def load_al():
+            nc.sync.dma_start(al8_sb[:], al8_words[0].rearrange("p n b -> p (n b)").bitcast(I32))
+            nc.sync.dma_start(al4_sb[:], al4_words[0].bitcast(I32))
+
+        def shift(g0, g1):
+            nc.sync.dma_start(shifted[0:112, g0:g1, :], plane[16:P, g0:g1, :])
 
         tab_planes = {}
         plane = sbuf([P, 2, K_PASS // 4], I32, "tab_plane")
@@ -106,39 +111,36 @@ def tile_list_kernl_tanh_mix_none_kernel(
 
         def pick_words(g):
             codes = sbuf([P, 2, K_PASS], U16, f"tab_codes{g}")
-            picked = sbuf([P, 2, K_PASS // 2], U32, f"picked_words{g}")
+            picked = [sbuf([P, K_PASS // 2], U32, f"picked_words{g}{h}") for h in range(2)]
             for h in range(2):
                 nc.vector.tensor_copy(
-                    picked[:, h, :].rearrange("p (t c) -> p c t", t=PACK),
+                    picked[h][:].rearrange("p (t c) -> p c t", t=PACK),
                     word_window[:].bitcast(U32).indirect(offsets[:, 32 * g + 16 * h : 32 * g + 16 * h + 16]),
                 )
             for h in range(2):
                 nc.vector.tensor_copy(
                     codes[:].rearrange("p a (t c) -> p a t c", t=PACK)[:, :, :, 64 * h : 64 * h + 64],
-                    picked[:, h, :].bitcast(U16).rearrange("p (t c a) -> p a t c", t=PACK, a=2),
+                    picked[h][:].bitcast(U16).rearrange("p (t c a) -> p a t c", t=PACK, a=2),
                 )
             tab_codes[g] = codes
 
         x_codes, x_scales, x_grouped = {}, {}, {}
 
         def round_x(a, c):
-            half = c // 2
-            key = (a, c) if half == 0 else (a, 2)
-            if key not in x_grouped:
-                width = PIECE if half == 0 else HALF
-                x_grouped[key] = sbuf([P, width * PACK], BF16, f"x_grouped{key[0]}{key[1]}")
-            lo = 0 if half == 0 else (c - 2) * PIECE * PACK
-            dst = x_grouped[key][:, lo : lo + PIECE * PACK].rearrange("p (c i t) -> p c t i", i=RUN, t=PACK)
-            src = x_raw[a, c][:, :, :].rearrange("p t (c i) -> p c t i", i=RUN)
+            c0 = FIRST[c]
+            if (a, c0) not in x_grouped:
+                x_grouped[a, c0] = sbuf([P, WIDTH[c0] * PACK], BF16, f"x_grouped{a}{c0}")
+            lo = (c - c0) * PIECE * PACK
+            dst = x_grouped[a, c0][:, lo : lo + PIECE * PACK].rearrange("p (c i t) -> p c t i", i=RUN, t=PACK)
+            src = x_raw[a, c].rearrange("p t (c i) -> p c t i", i=RUN)
             if (a, c) in VECTOR_CASTS:
                 nc.vector.tensor_copy(dst, src)
             else:
                 nc.scalar.copy(dst, src)
 
         def quantize_x(a, c):
-            width = PIECE if c < 2 else HALF
-            x_codes[a, c] = sbuf([P, width], U32, f"x_codes{a}{c}")
-            x_scales[a, c] = sbuf([P, width], U8, f"x_scales{a}{c}")
+            x_codes[a, c] = sbuf([P, WIDTH[c]], U32, f"x_codes{a}{c}")
+            x_scales[a, c] = sbuf([P, WIDTH[c]], U8, f"x_scales{a}{c}")
             nc.vector.quantize_mx(out=x_codes[a, c][:].bitcast(FP8X4), scales=x_scales[a, c][:], in_=x_grouped[a, c][:])
 
         def table_pass(dst, g, t, a, c, cols, start, stop):
@@ -155,7 +157,7 @@ def tile_list_kernl_tanh_mix_none_kernel(
         tanh_out = {}
 
         def kernel_values(g, c, n_cols, piece):
-            width = PIECE if c < 2 else HALF
+            width = WIDTH[c]
             th = sbuf([P, PACK, width], F32, f"tanh{g}{c}")
             banks = []
             for t in range(PACK):
@@ -176,7 +178,7 @@ def tile_list_kernl_tanh_mix_none_kernel(
         h_grouped = {}
 
         def weigh_h(g, m0, width):
-            c = min(m0 // PIECE, 2)
+            c = FIRST[m0 // PIECE]
             lo = m0 - c * PIECE
             grouped = sbuf([P, width * PACK], BF16, f"h_grouped{g}_{m0}")
             nc.vector.tensor_tensor(
@@ -214,15 +216,33 @@ def tile_list_kernl_tanh_mix_none_kernel(
             else:
                 nc.scalar.copy(dst, src)
 
-        def output_wide(m0):
+        def output_wide(m0, n, engine):
             cols = slice(m0, m0 + HALF)
+            y = psum.tile([P, HALF], F32, name="y")
+            for g in range(2):
+                output_pass(y[:], n, g, cols)
+            staged = sbuf([P, HALF], F32, f"y_wide{n}")
+            copy_out(engine, staged[:], y[:])
+            nc.sync.dma_start(out[n * P : (n + 1) * P, cols], staged[:])
+
+        open_banks = []
+
+        def open_last(m0):
             for n in range(N // P):
-                y = psum.tile([P, HALF], F32, name="y")
-                for g in range(2):
-                    output_pass(y[:], n, g, cols)
-                staged = sbuf([P, HALF], F32, f"y_wide{n}")
-                copy_out("s", staged[:], y[:])
-                nc.sync.dma_start(out[n * P : (n + 1) * P, cols], staged[:])
+                y = psum.tile([P, HALF], F32, name="d")
+                output_pass(y[:, :NARROW], n, 0, slice(m0, m0 + NARROW))
+                open_banks.append(y)
+
+        def close_last(m0):
+            for pair in range(2):
+                staged = sbuf([P, 2, NARROW], F32, f"y_last{pair}")
+                for i in range(2):
+                    y = open_banks[2 * pair + i]
+                    output_pass(y[:, :NARROW], 2 * pair + i, 1, slice(m0, m0 + NARROW))
+                    copy_out("vs"[i], staged[:, i, :], y[:, :NARROW])
+                nc.sync.dma_start(
+                    out[2 * pair * P : (2 * pair + 2) * P, m0 : m0 + NARROW].rearrange("(n p) m -> p n m", p=P), staged[:]
+                )
 
         def output_narrow(m0, width, n0, count, engine):
             y = psum.tile([P, HALF], F32, name="y")
@@ -237,9 +257,20 @@ def tile_list_kernl_tanh_mix_none_kernel(
                 out[n0 * P : (n0 + count) * P, m0 : m0 + width].rearrange("(n p) m -> p n m", p=P), staged[:]
             )
 
+        load_x(0, 0)
+        load_words()
+        load_x(1, 0)
+        load_x(0, 1)
+        load_cw()
         pick_scales(0)
         pick_scales(1)
-        nc.scalar.dma_start(shifted[0:112], plane[16:P])
+        shift(0, 2)
+        load_x(1, 1)
+        load_x(0, 2)
+        load_x(1, 2)
+        load_x(0, 3)
+        load_x(1, 3)
+        load_al()
         round_x(0, 0)
         quantize_x(0, 0)
         pick_words(0)
@@ -251,40 +282,48 @@ def tile_list_kernl_tanh_mix_none_kernel(
         round_x(0, 1)
         kernel_values(0, 0, NARROW, PIECE)
         pick_words(1)
+        kernel_values(1, 0, NARROW, PIECE)
         round_x(1, 1)
         quantize_x(0, 1)
         quantize_x(1, 1)
-        for c in (2, 3):
-            for a in range(2):
-                round_x(a, c)
-        quantize_x(0, 2)
-        quantize_x(1, 2)
-        kernel_values(1, 0, NARROW, PIECE)
         kernel_values(0, 1, NARROW, PIECE)
         kernel_values(1, 1, NARROW, PIECE)
-        kernel_values(0, 2, HALF, HALF)
-        kernel_values(1, 2, HALF, PIECE)
-        weigh_h(0, 0, PIECE)
-        weigh_h(1, 0, PIECE)
-        quantize_h(0, 0, PIECE)
-        weigh_h(0, PIECE, PIECE)
-        quantize_h(1, 0, PIECE)
-        weigh_h(1, PIECE, PIECE)
-        quantize_h(0, PIECE, PIECE)
-        quantize_h(1, PIECE, PIECE)
-        output_wide(0)
+        round_x(0, 2)
+        round_x(1, 2)
+        quantize_x(0, 2)
+        quantize_x(1, 2)
+        weigh_h(0, 0, 256)
+        weigh_h(1, 0, 256)
+        quantize_h(0, 0, 256)
+        quantize_h(1, 0, 256)
+        kernel_values(0, 2, NARROW, PIECE)
+        kernel_values(1, 2, NARROW, PIECE)
+        round_x(0, 3)
+        round_x(1, 3)
+        quantize_x(0, 3)
+        quantize_x(1, 3)
+        weigh_h(0, 256, 256)
+        weigh_h(1, 256, 256)
+        quantize_h(0, 256, 256)
+        quantize_h(1, 256, 256)
+        kernel_values(0, 3, NARROW, PIECE)
+        kernel_values(1, 3, NARROW, PIECE)
+        output_wide(0, 0, "s")
+        output_wide(0, 1, "s")
+        output_wide(0, 2, "s")
+        output_wide(0, 3, "s")
         weigh_h(0, 512, 256)
         weigh_h(1, 512, 256)
         quantize_h(0, 512, 256)
-        weigh_h(0, 768, 256)
         quantize_h(1, 512, 256)
         output_narrow(512, 256, 0, 2, "s")
         output_narrow(512, 256, 2, 2, "s")
+        weigh_h(0, 768, 256)
         weigh_h(1, 768, 128)
         quantize_h(0, 768, 256)
-        weigh_h(1, 896, 128)
         quantize_h(1, 768, 128)
         output_narrow(768, 128, 0, 4, "s")
+        open_last(896)
+        weigh_h(1, 896, 128)
         quantize_h(1, 896, 128)
-        output_narrow(896, 128, 0, 2, "v")
-        output_narrow(896, 128, 2, 2, "s")
+        close_last(896)

@@ -19,15 +19,10 @@ MULT = mybir.AluOpType.mult
 P = 128
 PACK = 4
 K_PASS = P * PACK
-HALF = 512
+BANK = 512
 PIECE = 256
 RUN = 2
 NARROW = 128
-VECTOR_CASTS = {(1, 1), (1, 2), (0, 3), (1, 3)}
-WARM_PASSES = 4
-WIDTH = {0: 256, 1: 256, 2: 256, 3: 256}
-FIRST = (0, 1, 2, 3)
-AFTER = {"picked_words10":"picked_words00","picked_words11":"x_raw10","h_grouped1_896":"h_grouped0_768"}
 
 
 def tile_list_kernl_tanh_mix_none_kernel(
@@ -37,165 +32,187 @@ def tile_list_kernl_tanh_mix_none_kernel(
     with ExitStack() as ctx:
         keep = ctx.enter_context(tc.tile_pool(name="keep", bufs=1))
         share = ctx.enter_context(tc.tile_pool(name="share", bufs=1))
-        psum = ctx.enter_context(tc.psum_pool(name="psum", bufs=4))
+        psum = ctx.enter_context(tc.psum_pool(name="psum", bufs=1))
 
-        def sbuf(shape, dtype, name):
-            return share.tile(shape, dtype, name=name, tag=AFTER.get(name, name), align_bytes=64)
+        def sbuf(shape, dtype, name, slot=None):
+            return share.tile(shape, dtype, name=name, tag=slot or name, align_bytes=64)
+
+        def bank(index, name):
+            return psum.tile([P, BANK], F32, name=name, tag=f"bank{index}")
 
         offsets = keep.tile([P, J // 16], U16, name="offsets")
-        nc.sync.dma_start(offsets[:], offs)
-
         scale_window = sbuf([P, T // 4], I32, "scale_window")
-        nc.vector.memset(scale_window[:], 0)
-        warm_in = sbuf([P, 1], F32, "warm_in")
-        nc.vector.memset(warm_in[:], 0.0)
-        warm_out = sbuf([P, 1], F32, "warm_out")
-        nc.scalar.activation(out=warm_out[:], in_=warm_in[:], func=TANH)
-        shifted = sbuf([P, 2, K_PASS // 4], I32, "shifted")
-        nc.vector.memset(shifted[:], 0)
-        al_planes = sbuf([P, 2, N // 4], I32, "al_planes")
-        nc.gpsimd.memset(al_planes[:], 0)
-
-        cb_sb = sbuf([P, 2, PACK], F32, "cb_sb")
-        nc.sync.dma_start(cb_sb[:], cb.rearrange("(g p t) -> p g t", g=2, t=PACK))
-        scale_rows = tab_scales.bitcast(I32).rearrange("a (q r) w -> r q a w", r=4)
-        for r in range(4):
-            nc.sync.dma_start(scale_window[r:P:16, :], scale_rows[r])
-
-        for g, scales in enumerate((al8_scales, al4_scales)):
-            for q in range(4):
-                nc.gpsimd.dma_start(al_planes[32 * q : 32 * q + 4, g, :], scales[0, 4 * q : 4 * q + 4, :].bitcast(I32))
-
-        x_raw = {}
-
-        def load_x(a, c0, count=1):
-            raw = sbuf([P, PACK, count * PIECE], F32, f"x_raw{a}{c0}")
-            rows = x[a * K_PASS : (a + 1) * K_PASS, c0 * PIECE : (c0 + count) * PIECE]
-            nc.sync.dma_start(raw[:], rows.rearrange("(p i) w -> p i w", i=PACK))
-            for c in range(count):
-                x_raw[a, c0 + c] = raw[:, :, c * PIECE : (c + 1) * PIECE]
-
         word_window = sbuf([P, T], I32, "word_window")
+        cb_sb = sbuf([P, 2, PACK], F32, "cb_sb")
+        cw_sb = sbuf([P, 2, PACK], F32, "cw_sb")
+        al8_sb = sbuf([P, N], I32, "al8_sb")
+        al4_sb = sbuf([P, N // 2], I32, "al4_sb")
+        al_planes = sbuf([P, 2, N // 4], I32, "al_planes")
+        x_codes = [sbuf([P, M], U32, f"x_codes{a}") for a in range(2)]
+        x_scales = [sbuf([P, M], U8, f"x_scales{a}") for a in range(2)]
+        h_codes = [sbuf([P, M], U32, f"h_codes{g}") for g in range(2)]
+        h_scales = [sbuf([P, M], U8, f"h_scales{g}") for g in range(2)]
+        x_raw, x_grouped, tab_codes, tab_planes, sums, tanh_out, h_grouped, y_banks = {}, {}, {}, {}, {}, {}, {}, {}
+
+        def warm_up():
+            warm_in = sbuf([P, 1], F32, "warm_in")
+            nc.vector.memset(warm_in[:], 0.0)
+            warm_out = sbuf([P, 1], F32, "warm_out")
+            nc.scalar.activation(out=warm_out[:], in_=warm_in[:], func=TANH)
+
+        def load_scale_rows(queue):
+            nc.vector.memset(scale_window[:], 0)
+            rows = tab_scales.bitcast(I32).rearrange("a (q r) w -> r q a w", r=4)
+            for r in range(4):
+                queue.dma_start(scale_window[r:P:16, :], rows[r])
 
         def load_words():
             nc.sync.dma_start(word_window[:], tab_words[0].rearrange("p t b -> p (t b)").bitcast(I32))
 
-        cw_sb = sbuf([P, 2, PACK], F32, "cw_sb")
-        al8_sb = sbuf([P, N], I32, "al8_sb")
-        al4_sb = sbuf([P, N // 2], I32, "al4_sb")
+        def load_x(a, m0, width):
+            raw = sbuf([P, PACK, width], F32, f"x_raw{a}_{m0}")
+            rows = x[a * K_PASS : (a + 1) * K_PASS, m0 : m0 + width]
+            nc.sync.dma_start(raw[:], rows.rearrange("(p i) w -> p i w", i=PACK))
+            for lo in range(0, width, NARROW):
+                x_raw[a, m0 + lo] = (raw, lo)
 
-        def load_cw():
-            nc.gpsimd.dma_start(cw_sb[:], cw.rearrange("(g p t) -> p g t", g=2, t=PACK))
+        def load_vector(queue, tile, vector):
+            queue.dma_start(tile[:], vector.rearrange("(g p t) -> p g t", g=2, t=PACK))
 
-        def load_al():
+        def load_al(queue):
             nc.sync.dma_start(al8_sb[:], al8_words[0].rearrange("p n b -> p (n b)").bitcast(I32))
             nc.sync.dma_start(al4_sb[:], al4_words[0].bitcast(I32))
 
-        def shift(g0, g1):
-            nc.sync.dma_start(shifted[0:112, g0:g1, :], plane[16:P, g0:g1, :])
+        def load_al_scales(queue):
+            for g, scales in enumerate((al8_scales, al4_scales)):
+                for q in range(4):
+                    queue.dma_start(al_planes[32 * q : 32 * q + 4, g, :], scales[0, 4 * q : 4 * q + 4, :].bitcast(I32))
 
-        tab_planes = {}
-        plane = sbuf([P, 2, K_PASS // 4], I32, "tab_plane")
+        picked_scales = sbuf([P, J], U8, "picked_scales")
+        plane = sbuf([P, J // 4], I32, "tab_plane")
 
-        def pick_scales(g):
-            picked = sbuf([P, K_PASS], U8, f"picked_scales{g}")
-            nc.vector.tensor_copy(picked[:], scale_window[:].bitcast(U8).indirect(offsets[:, 32 * g : 32 * g + 32]))
+        def pick_scales(j0, count):
             nc.vector.tensor_copy(
-                plane[:, g, :].bitcast(U8).rearrange("p (t c) -> p t c", t=PACK),
-                picked[:].rearrange("p (c t) -> p t c", t=PACK),
+                picked_scales[:, j0 : j0 + count],
+                scale_window[:].bitcast(U8).indirect(offsets[:, j0 // 16 : (j0 + count) // 16]),
             )
-            tab_planes[g, 0] = plane[:, g, :].bitcast(U8)
-            tab_planes[g, 1] = shifted[:, g, :].bitcast(U8)
 
-        tab_codes = {}
+        def order_scales(g0, g1):
+            cols = slice(g0 * K_PASS, g1 * K_PASS)
+            nc.vector.tensor_copy(
+                plane[:].bitcast(U8)[:, cols].rearrange("p (g t c) -> p g t c", t=PACK, c=P),
+                picked_scales[:, cols].rearrange("p (g c t) -> p g t c", t=PACK, c=P),
+            )
 
-        def pick_words(g):
-            codes = sbuf([P, 2, K_PASS], U16, f"tab_codes{g}")
-            picked = [sbuf([P, K_PASS // 2], U32, f"picked_words{g}{h}") for h in range(2)]
-            for h in range(2):
-                nc.vector.tensor_copy(
-                    picked[h][:].rearrange("p (t c) -> p c t", t=PACK),
-                    word_window[:].bitcast(U32).indirect(offsets[:, 32 * g + 16 * h : 32 * g + 16 * h + 16]),
-                )
-            for h in range(2):
-                nc.vector.tensor_copy(
-                    codes[:].rearrange("p a (t c) -> p a t c", t=PACK)[:, :, :, 64 * h : 64 * h + 64],
-                    picked[h][:].bitcast(U16).rearrange("p (t c a) -> p a t c", t=PACK, a=2),
-                )
-            tab_codes[g] = codes
+        shifted = sbuf([P, J // 4], I32, "shifted")
+        tab_planes[0] = plane[:].bitcast(U8)
+        tab_planes[1] = shifted[:].bitcast(U8)
 
-        x_codes, x_scales, x_grouped = {}, {}, {}
+        def shift_scales(queue, g0, g1):
+            cols = slice(g0 * P, g1 * P)
+            queue.dma_start(shifted[0:112, cols], plane[16:P, cols])
 
-        def round_x(a, c):
-            c0 = FIRST[c]
-            if (a, c0) not in x_grouped:
-                x_grouped[a, c0] = sbuf([P, WIDTH[c0] * PACK], BF16, f"x_grouped{a}{c0}")
-            lo = (c - c0) * PIECE * PACK
-            dst = x_grouped[a, c0][:, lo : lo + PIECE * PACK].rearrange("p (c i t) -> p c t i", i=RUN, t=PACK)
-            src = x_raw[a, c].rearrange("p t (c i) -> p c t i", i=RUN)
-            if (a, c) in VECTOR_CASTS:
+        picked_words = {}
+        for g in range(2):
+            tab_codes[g] = sbuf([P, 2, K_PASS], U16, f"tab_codes{g}")
+
+        def pick_words(g, half, slot=None):
+            picked = sbuf([P, K_PASS // 2], U32, f"picked_words{g}{half}", slot)
+            j0 = g * K_PASS + half * K_PASS // 2
+            nc.vector.tensor_copy(
+                picked[:].rearrange("p (t c) -> p c t", t=PACK),
+                word_window[:].bitcast(U32).indirect(offsets[:, j0 // 16 : j0 // 16 + K_PASS // 32]),
+            )
+            picked_words[g, half] = picked
+
+        def part_words(g, half):
+            nc.vector.tensor_copy(
+                tab_codes[g][:].rearrange("p a (t c) -> p a t c", t=PACK)[:, :, :, 64 * half : 64 * half + 64],
+                picked_words[g, half][:].bitcast(U16).rearrange("p (t c a) -> p a t c", t=PACK, a=2),
+            )
+
+        def round_x(a, m0, width, engine, slot=None):
+            raw, lo = x_raw[a, m0]
+            grouped = sbuf([P, width * PACK], BF16, f"x_grouped{a}_{m0}", slot)
+            dst = grouped[:].rearrange("p (c i t) -> p c t i", i=RUN, t=PACK)
+            src = raw[:, :, lo : lo + width].rearrange("p t (c i) -> p c t i", i=RUN)
+            if engine == "v":
                 nc.vector.tensor_copy(dst, src)
             else:
                 nc.scalar.copy(dst, src)
+            x_grouped[a, m0] = (grouped, width)
 
-        def quantize_x(a, c):
-            x_codes[a, c] = sbuf([P, WIDTH[c]], U32, f"x_codes{a}{c}")
-            x_scales[a, c] = sbuf([P, WIDTH[c]], U8, f"x_scales{a}{c}")
-            nc.vector.quantize_mx(out=x_codes[a, c][:].bitcast(FP8X4), scales=x_scales[a, c][:], in_=x_grouped[a, c][:])
+        def quantize_x(a, m0):
+            grouped, width = x_grouped[a, m0]
+            cols = slice(m0, m0 + width)
+            nc.vector.quantize_mx(out=x_codes[a][:, cols].bitcast(FP8X4), scales=x_scales[a][:, cols], in_=grouped[:])
 
-        def table_pass(dst, g, t, a, c, cols, start, stop):
+        def table_pass(dst, g, t, a, cols, start, stop):
             nc.tensor.matmul_mx(
                 out=dst,
                 lhsT=tab_codes[g][:, a, t * P : (t + 1) * P].bitcast(FP4X4),
-                lhsT_scale=tab_planes[g, a][:, t * P : (t + 1) * P],
-                rhs=x_codes[a, c][:, cols].bitcast(FP8X4),
-                rhs_scale=x_scales[a, c][:, cols],
+                lhsT_scale=tab_planes[a][:, g * K_PASS + t * P : g * K_PASS + (t + 1) * P],
+                rhs=x_codes[a][:, cols].bitcast(FP8X4),
+                rhs_scale=x_scales[a][:, cols],
                 start=start,
                 stop=stop,
             )
 
-        tanh_out = {}
-
-        def kernel_values(g, c, n_cols, piece):
-            width = WIDTH[c]
-            th = sbuf([P, PACK, width], F32, f"tanh{g}{c}")
-            banks = []
+        def narrow_sums(g, m0, width, banks):
+            per_bank = PACK // len(banks)
             for t in range(PACK):
-                d = psum.tile([P, HALF], F32, name="d")
-                for lo in range(0, width, n_cols):
-                    for a in range(2):
-                        table_pass(d[:, lo : lo + n_cols], g, t, a, c, slice(lo, lo + n_cols), a == 0, a == 1)
-                banks.append(d)
-            for lo in range(0, width, piece):
-                for t in range(PACK):
-                    nc.scalar.activation(
-                        out=th[:, t, lo : lo + piece], in_=banks[t][:, lo : lo + piece], func=TANH, bias=cb_sb[:, g, t : t + 1]
-                    )
-            tanh_out[g, c] = th
+                if t % per_bank == 0:
+                    d = bank(banks[t // per_bank], f"d{g}_{m0}_{t}")
+                base = (t % per_bank) * width
+                for a in range(2):
+                    for lo in range(0, width, NARROW):
+                        first, last = a == 0 and lo == 0, a == 1 and lo + NARROW == width
+                        table_pass(d[:, base + lo : base + lo + NARROW], g, t, a, slice(m0 + lo, m0 + lo + NARROW), first, last)
+                sums[g, m0, t] = d[:, base : base + width]
 
-        h_codes = [sbuf([P, M], U32, f"h_codes{g}") for g in range(2)]
-        h_scales = [sbuf([P, M], U8, f"h_scales{g}") for g in range(2)]
-        h_grouped = {}
+        def open_wide(g, m0, banks):
+            for t in range(PACK):
+                d = bank(banks[t], f"d{g}_{m0}_{t}")
+                table_pass(d[:], g, t, 0, slice(m0, m0 + BANK), True, False)
+                sums[g, m0, t] = d[:]
 
-        def weigh_h(g, m0, width):
-            c = FIRST[m0 // PIECE]
-            lo = m0 - c * PIECE
-            grouped = sbuf([P, width * PACK], BF16, f"h_grouped{g}_{m0}")
+        def close_wide(g, m0):
+            for t in range(PACK):
+                table_pass(sums[g, m0, t], g, t, 1, slice(m0, m0 + BANK), False, True)
+
+        def wide_sums(g, m0, banks):
+            for t in range(PACK):
+                d = bank(banks[t], f"d{g}_{m0}_{t}")
+                for a in range(2):
+                    table_pass(d[:], g, t, a, slice(m0, m0 + BANK), a == 0, a == 1)
+                sums[g, m0, t] = d[:]
+
+        def tanh(g, m0, lo, width):
+            th = sbuf([P, PACK, width], F32, f"tanh{g}_{m0 + lo}")
+            for t in range(PACK):
+                nc.scalar.activation(
+                    out=th[:, t, :], in_=sums[g, m0, t][:, lo : lo + width], func=TANH, bias=cb_sb[:, g, t : t + 1]
+                )
+            for k in range(0, width, NARROW):
+                tanh_out[g, m0 + lo + k] = (th, k)
+
+        def weigh_h(g, m0, width, slot=None):
+            th, lo = tanh_out[g, m0]
+            grouped = sbuf([P, width * PACK], BF16, f"h_grouped{g}_{m0}", slot)
             nc.vector.tensor_tensor(
                 grouped[:].rearrange("p (c i t) -> p c t i", i=RUN, t=PACK),
-                tanh_out[g, c][:, :, lo : lo + width].rearrange("p t (c i) -> p c t i", i=RUN),
+                th[:, :, lo : lo + width].rearrange("p t (c i) -> p c t i", i=RUN),
                 cw_sb[:, g, :].rearrange("p (c t i) -> p c t i", c=1, i=1).to_broadcast([P, width // RUN, PACK, RUN]),
                 MULT,
             )
-            h_grouped[g, m0] = grouped
+            h_grouped[g, m0] = (grouped, width)
 
-        def quantize_h(g, m0, width):
+        def quantize_h(g, m0):
+            grouped, width = h_grouped[g, m0]
             cols = slice(m0, m0 + width)
-            nc.vector.quantize_mx(
-                out=h_codes[g][:, cols].bitcast(FP8X4), scales=h_scales[g][:, cols], in_=h_grouped[g, m0][:]
-            )
+            nc.vector.quantize_mx(out=h_codes[g][:, cols].bitcast(FP8X4), scales=h_scales[g][:, cols], in_=grouped[:])
 
-        def output_pass(dst, n, g, cols):
+        def output_pass(dst, n, g, cols, start, stop):
             if g == 0:
                 weights = al8_sb[:, n * P : (n + 1) * P].bitcast(FP8X4)
             else:
@@ -206,124 +223,157 @@ def tile_list_kernl_tanh_mix_none_kernel(
                 lhsT_scale=al_planes[:, g, :].bitcast(U8)[:, n * P : (n + 1) * P],
                 rhs=h_codes[g][:, cols].bitcast(FP8X4),
                 rhs_scale=h_scales[g][:, cols],
-                start=(g == 0),
-                stop=(g == 1),
+                start=start,
+                stop=stop,
             )
 
-        def copy_out(engine, dst, src):
-            if engine == "v":
-                nc.vector.tensor_copy(dst, src)
-            else:
-                nc.scalar.copy(dst, src)
-
-        def output_wide(m0, n, engine):
-            cols = slice(m0, m0 + HALF)
-            y = psum.tile([P, HALF], F32, name="y")
-            for g in range(2):
-                output_pass(y[:], n, g, cols)
-            staged = sbuf([P, HALF], F32, f"y_wide{n}")
-            copy_out(engine, staged[:], y[:])
-            nc.sync.dma_start(out[n * P : (n + 1) * P, cols], staged[:])
-
-        open_banks = []
-
-        def open_last(m0):
-            for n in range(N // P):
-                y = psum.tile([P, HALF], F32, name="d")
-                output_pass(y[:, :NARROW], n, 0, slice(m0, m0 + NARROW))
-                open_banks.append(y)
-
-        def close_last(m0):
-            for pair in range(2):
-                staged = sbuf([P, 2, NARROW], F32, f"y_last{pair}")
-                for i in range(2):
-                    y = open_banks[2 * pair + i]
-                    output_pass(y[:, :NARROW], 2 * pair + i, 1, slice(m0, m0 + NARROW))
-                    copy_out("vs"[i], staged[:, i, :], y[:, :NARROW])
-                nc.sync.dma_start(
-                    out[2 * pair * P : (2 * pair + 2) * P, m0 : m0 + NARROW].rearrange("(n p) m -> p n m", p=P), staged[:]
-                )
-
-        def output_narrow(m0, width, n0, count, engine):
-            y = psum.tile([P, HALF], F32, name="y")
+        def output_sums(m0, width, n0, count, index):
+            y = bank(index, f"y{m0}_{n0}")
             for i in range(count):
-                for lo in range(0, width, NARROW):
-                    for g in range(2):
-                        dst = y[:, i * width + lo : i * width + lo + NARROW]
-                        output_pass(dst, n0 + i, g, slice(m0 + lo, m0 + lo + NARROW))
-            staged = sbuf([P, count, width], F32, f"y_narrow{m0}_{n0}")
-            copy_out(engine, staged[:].rearrange("p n m -> p (n m)"), y[:, : count * width])
-            nc.sync.dma_start(
-                out[n0 * P : (n0 + count) * P, m0 : m0 + width].rearrange("(n p) m -> p n m", p=P), staged[:]
+                base = i * width
+                output_pass(y[:, base : base + width], n0 + i, 0, slice(m0, m0 + width), True, False)
+                step = width if width == BANK else NARROW
+                for lo in range(0, width, step):
+                    output_pass(
+                        y[:, base + lo : base + lo + step], n0 + i, 1, slice(m0 + lo, m0 + lo + step), False, lo + step == width
+                    )
+            y_banks[m0, n0] = (y, width, count)
+
+        def open_output(m0, width, banks):
+            for n in range(N // P):
+                y = bank(banks[n], f"y{m0}_{n}")
+                output_pass(y[:, :width], n, 0, slice(m0, m0 + width), True, False)
+                y_banks[m0, n] = (y, width, 1)
+
+        def close_output(m0, n):
+            y, width, count = y_banks[m0, n]
+            output_pass(y[:, :width], n, 1, slice(m0, m0 + width), False, True)
+
+        def store_rows(m0, n0, engines, queue):
+            width = y_banks[m0, n0][1]
+            staged = sbuf([P, len(engines), width], F32, f"y_staged{m0}_{n0}")
+            for i, engine in enumerate(engines):
+                y = y_banks[m0, n0 + i][0]
+                if engine == "v":
+                    nc.vector.tensor_copy(staged[:, i, :], y[:, :width])
+                else:
+                    nc.scalar.copy(staged[:, i, :], y[:, :width])
+            queue.dma_start(
+                out[n0 * P : (n0 + len(engines)) * P, m0 : m0 + width].rearrange("(n p) m -> p n m", p=P), staged[:]
             )
 
-        load_x(0, 0)
+        def store(m0, n0, engine, queue):
+            y, width, count = y_banks[m0, n0]
+            staged = sbuf([P, count * width], F32, f"y_staged{m0}_{n0}")
+            if engine == "v":
+                nc.vector.tensor_copy(staged[:], y[:, : count * width])
+            else:
+                nc.scalar.copy(staged[:], y[:, : count * width])
+            queue.dma_start(
+                out[n0 * P : (n0 + count) * P, m0 : m0 + width].rearrange("(n p) m -> p n m", p=P),
+                staged[:].rearrange("p (n m) -> p n m", n=count),
+            )
+
+        nc.sync.dma_start(offsets[:], offs)
+        load_vector(nc.sync, cb_sb, cb)
+        load_scale_rows(nc.sync)
         load_words()
-        load_x(1, 0)
-        load_x(0, 1)
-        load_cw()
-        pick_scales(0)
-        pick_scales(1)
-        shift(0, 2)
-        load_x(1, 1)
-        load_x(0, 2)
-        load_x(1, 2)
-        load_x(0, 3)
-        load_x(1, 3)
-        load_al()
-        round_x(0, 0)
+        load_x(0, 0, 256)
+        load_x(1, 0, 256)
+        load_vector(nc.gpsimd, cw_sb, cw)
+        warm_up()
+        nc.vector.memset(shifted[96:P, :], 0)
+        nc.gpsimd.memset(al_planes[:], 0)
+        load_al_scales(nc.gpsimd)
+        pick_scales(0, 512)
+        pick_scales(512, 512)
+        order_scales(0, 1)
+        order_scales(1, 2)
+        load_x(0, 256, 256)
+        shift_scales(nc.sync, 0, 2)
+        load_x(1, 256, 256)
+        load_x(0, 512, 256)
+        load_x(1, 512, 256)
+        load_x(0, 768, 256)
+        load_x(1, 768, 256)
+        load_al(nc.sync)
+        pick_words(0, 0)
+        pick_words(0, 1)
+        part_words(0, 0)
+        part_words(0, 1)
+        round_x(0, 0, 256, "s")
+        round_x(1, 0, 256, "s")
         quantize_x(0, 0)
-        pick_words(0)
-        round_x(1, 0)
+        pick_words(1, 0, "x_raw0_0")
         quantize_x(1, 0)
-        for w in range(WARM_PASSES):
-            warm = psum.tile([P, HALF], F32, name="y")
-            table_pass(warm[:, :PIECE], 0, w % PACK, 0, 0, slice(0, PIECE), True, True)
-        round_x(0, 1)
-        kernel_values(0, 0, NARROW, PIECE)
-        pick_words(1)
-        kernel_values(1, 0, NARROW, PIECE)
-        round_x(1, 1)
-        quantize_x(0, 1)
-        quantize_x(1, 1)
-        kernel_values(0, 1, NARROW, PIECE)
-        kernel_values(1, 1, NARROW, PIECE)
-        round_x(0, 2)
-        round_x(1, 2)
-        quantize_x(0, 2)
-        quantize_x(1, 2)
+        pick_words(1, 1, "x_raw1_0")
+        narrow_sums(0, 0, 256, (0, 1, 2, 3))
+        round_x(0, 256, 256, "s")
+        part_words(1, 0)
+        part_words(1, 1)
+        tanh(0, 0, 0, 256)
+        round_x(1, 256, 256, "v")
+        narrow_sums(1, 0, 256, (4, 5))
+        quantize_x(0, 256)
+        quantize_x(1, 256)
+        narrow_sums(0, 256, 256, (6, 7))
+        narrow_sums(1, 256, 256, (0, 1))
+        round_x(0, 512, 256, "s")
+        tanh(1, 0, 0, 256)
         weigh_h(0, 0, 256)
+        round_x(1, 512, 256, "v")
+        tanh(0, 256, 0, 256)
+        quantize_x(0, 512)
+        quantize_x(1, 512)
+        narrow_sums(0, 512, 256, (2, 3))
+        narrow_sums(1, 512, 256, (4, 5))
+        tanh(1, 256, 0, 256)
         weigh_h(1, 0, 256)
-        quantize_h(0, 0, 256)
-        quantize_h(1, 0, 256)
-        kernel_values(0, 2, NARROW, PIECE)
-        kernel_values(1, 2, NARROW, PIECE)
-        round_x(0, 3)
-        round_x(1, 3)
-        quantize_x(0, 3)
-        quantize_x(1, 3)
+        quantize_h(0, 0)
+        round_x(0, 768, 256, "v")
+        quantize_h(1, 0)
+        round_x(1, 768, 256, "v")
+        output_sums(0, 256, 0, 2, 6)
+        output_sums(0, 256, 2, 2, 7)
+        tanh(0, 512, 0, 256)
+        quantize_x(0, 768)
+        quantize_x(1, 768)
+        narrow_sums(0, 768, 256, (0, 1))
+        narrow_sums(1, 768, 256, (2, 3))
         weigh_h(0, 256, 256)
         weigh_h(1, 256, 256)
-        quantize_h(0, 256, 256)
-        quantize_h(1, 256, 256)
-        kernel_values(0, 3, NARROW, PIECE)
-        kernel_values(1, 3, NARROW, PIECE)
-        output_wide(0, 0, "s")
-        output_wide(0, 1, "s")
-        output_wide(0, 2, "s")
-        output_wide(0, 3, "s")
+        tanh(1, 512, 0, 256)
+        store(0, 0, "s", nc.sync)
+        store(0, 2, "s", nc.sync)
+        quantize_h(0, 256)
+        quantize_h(1, 256)
+        output_sums(256, 256, 0, 2, 4)
+        output_sums(256, 256, 2, 2, 5)
+        tanh(0, 768, 0, 256)
         weigh_h(0, 512, 256)
         weigh_h(1, 512, 256)
-        quantize_h(0, 512, 256)
-        quantize_h(1, 512, 256)
-        output_narrow(512, 256, 0, 2, "s")
-        output_narrow(512, 256, 2, 2, "s")
+        tanh(1, 768, 0, 256)
+        store(256, 0, "s", nc.sync)
+        store(256, 2, "s", nc.sync)
+        quantize_h(0, 512)
+        quantize_h(1, 512)
+        output_sums(512, 256, 0, 2, 6)
+        output_sums(512, 256, 2, 2, 7)
         weigh_h(0, 768, 256)
         weigh_h(1, 768, 128)
-        quantize_h(0, 768, 256)
-        quantize_h(1, 768, 128)
-        output_narrow(768, 128, 0, 4, "s")
-        open_last(896)
+        store(512, 0, "s", nc.sync)
+        store(512, 2, "s", nc.sync)
+        quantize_h(0, 768)
+        open_output(768, 128, (0, 1, 2, 3))
+        quantize_h(1, 768)
+        for n in range(4):
+            close_output(768, n)
+        open_output(896, 128, (4, 5, 6, 7))
         weigh_h(1, 896, 128)
-        quantize_h(1, 896, 128)
-        close_last(896)
+        quantize_h(1, 896)
+        store_rows(768, 0, "ss", nc.sync)
+        store_rows(768, 2, "ss", nc.sync)
+        for n in range(4):
+            close_output(896, n)
+        store_rows(896, 0, "vs", nc.sync)
+        store_rows(896, 2, "vs", nc.sync)

@@ -18,11 +18,19 @@ MULT = mybir.AluOpType.mult
 
 P = 128
 PACK = 4
-K_PASS = P * PACK
+PASS = P * PACK
+PASSES = K // PASS
+GROUPS = J // PASS
+LIST_ROWS = 16
 BANK = 512
+BANKS = 8
 PIECE = 256
-RUN = 2
+PIECES = M // PIECE
 NARROW = 128
+RUN = 2
+SHIFT = 16
+
+SCALAR_ROUNDS = {(0, 0): PIECE, (1, 0): PIECE, (0, 1): PIECE, (0, 3): PIECE // 2}
 
 
 def tile_list_kernl_tanh_mix_none_kernel(
@@ -34,346 +42,270 @@ def tile_list_kernl_tanh_mix_none_kernel(
         share = ctx.enter_context(tc.tile_pool(name="share", bufs=1))
         psum = ctx.enter_context(tc.psum_pool(name="psum", bufs=1))
 
-        def sbuf(shape, dtype, name, slot=None):
-            return share.tile(shape, dtype, name=name, tag=slot or name, align_bytes=64)
+        def sbuf(shape, dtype, name, reuse=None):
+            return share.tile(shape, dtype, name=name, tag=reuse or name, align_bytes=64)
 
-        def bank(index, name):
-            return psum.tile([P, BANK], F32, name=name, tag=f"bank{index}")
+        handed_out = []
 
-        offsets = keep.tile([P, J // 16], U16, name="offsets")
-        scale_window = sbuf([P, T // 4], I32, "scale_window")
-        word_window = sbuf([P, T], I32, "word_window")
-        cb_sb = sbuf([P, 2, PACK], F32, "cb_sb")
-        cw_sb = sbuf([P, 2, PACK], F32, "cw_sb")
-        al8_sb = sbuf([P, N], I32, "al8_sb")
-        al4_sb = sbuf([P, N // 2], I32, "al4_sb")
-        al_planes = sbuf([P, 2, N // 4], I32, "al_planes")
-        x_codes = [sbuf([P, M], U32, f"x_codes{a}") for a in range(2)]
-        x_scales = [sbuf([P, M], U8, f"x_scales{a}") for a in range(2)]
-        h_codes = [sbuf([P, M], U32, f"h_codes{g}") for g in range(2)]
-        h_scales = [sbuf([P, M], U8, f"h_scales{g}") for g in range(2)]
-        x_raw, x_grouped, tab_codes, tab_planes, sums, tanh_out, h_grouped, y_banks = {}, {}, {}, {}, {}, {}, {}, {}
+        def next_bank(name):
+            handed_out.append(name)
+            return psum.tile([P, BANK], F32, name=name, tag=f"bank{(len(handed_out) - 1) % BANKS}")
 
-        def warm_up():
-            warm_in = sbuf([P, 1], F32, "warm_in")
-            nc.vector.memset(warm_in[:], 0.0)
-            warm_out = sbuf([P, 1], F32, "warm_out")
-            nc.scalar.activation(out=warm_out[:], in_=warm_in[:], func=TANH)
-
-        def load_scale_rows(queue):
-            nc.vector.memset(scale_window[:], 0)
-            rows = tab_scales.bitcast(I32).rearrange("a (q r) w -> r q a w", r=4)
-            for r in range(4):
-                queue.dma_start(scale_window[r:P:16, :], rows[r])
-
-        def load_words():
-            nc.sync.dma_start(word_window[:], tab_words[0].rearrange("p t b -> p (t b)").bitcast(I32))
-
-        def load_x(a, m0, width):
-            raw = sbuf([P, PACK, width], F32, f"x_raw{a}_{m0}")
-            rows = x[a * K_PASS : (a + 1) * K_PASS, m0 : m0 + width]
-            nc.sync.dma_start(raw[:], rows.rearrange("(p i) w -> p i w", i=PACK))
-            for lo in range(0, width, NARROW):
-                x_raw[a, m0 + lo] = (raw, lo)
-
-        def load_vector(queue, tile, vector):
-            queue.dma_start(tile[:], vector.rearrange("(g p t) -> p g t", g=2, t=PACK))
-
-        def load_al(queue):
-            nc.sync.dma_start(al8_sb[:], al8_words[0].rearrange("p n b -> p (n b)").bitcast(I32))
-            nc.sync.dma_start(al4_sb[:], al4_words[0].bitcast(I32))
-
-        def load_al_scales(queue):
-            for g, scales in enumerate((al8_scales, al4_scales)):
-                for q in range(4):
-                    queue.dma_start(al_planes[32 * q : 32 * q + 4, g, :], scales[0, 4 * q : 4 * q + 4, :].bitcast(I32))
-
-        picked_scales = sbuf([P, J], U8, "picked_scales")
-        plane = sbuf([P, J // 4], I32, "tab_plane")
-
-        def pick_scales(j0, count):
-            nc.vector.tensor_copy(
-                picked_scales[:, j0 : j0 + count],
-                scale_window[:].bitcast(U8).indirect(offsets[:, j0 // 16 : (j0 + count) // 16]),
-            )
-
-        def order_scales(g0, g1):
-            cols = slice(g0 * K_PASS, g1 * K_PASS)
-            nc.vector.tensor_copy(
-                plane[:].bitcast(U8)[:, cols].rearrange("p (g t c) -> p g t c", t=PACK, c=P),
-                picked_scales[:, cols].rearrange("p (g c t) -> p g t c", t=PACK, c=P),
-            )
-
-        shifted = sbuf([P, J // 4], I32, "shifted")
-        tab_planes[0] = plane[:].bitcast(U8)
-        tab_planes[1] = shifted[:].bitcast(U8)
-
-        def shift_scales(queue, g0, g1):
-            cols = slice(g0 * P, g1 * P)
-            queue.dma_start(shifted[0:112, cols], plane[16:P, cols])
-
-        picked_words = {}
-        for g in range(2):
-            tab_codes[g] = sbuf([P, 2, K_PASS], U16, f"tab_codes{g}")
-
-        def pick_words(g, half, slot=None):
-            picked = sbuf([P, K_PASS // 2], U32, f"picked_words{g}{half}", slot)
-            j0 = g * K_PASS + half * K_PASS // 2
-            nc.vector.tensor_copy(
-                picked[:].rearrange("p (t c) -> p c t", t=PACK),
-                word_window[:].bitcast(U32).indirect(offsets[:, j0 // 16 : j0 // 16 + K_PASS // 32]),
-            )
-            picked_words[g, half] = picked
-
-        def part_words(g, half):
-            nc.vector.tensor_copy(
-                tab_codes[g][:].rearrange("p a (t c) -> p a t c", t=PACK)[:, :, :, 64 * half : 64 * half + 64],
-                picked_words[g, half][:].bitcast(U16).rearrange("p (t c a) -> p a t c", t=PACK, a=2),
-            )
-
-        def round_x(a, m0, width, engine, slot=None):
-            raw, lo = x_raw[a, m0]
-            grouped = sbuf([P, width * PACK], BF16, f"x_grouped{a}_{m0}", slot)
-            dst = grouped[:].rearrange("p (c i t) -> p c t i", i=RUN, t=PACK)
-            src = raw[:, :, lo : lo + width].rearrange("p t (c i) -> p c t i", i=RUN)
-            if engine == "v":
+        def copy(engine, dst, src):
+            if engine is nc.vector:
                 nc.vector.tensor_copy(dst, src)
             else:
                 nc.scalar.copy(dst, src)
-            x_grouped[a, m0] = (grouped, width)
 
-        def quantize_x(a, m0):
-            grouped, width = x_grouped[a, m0]
-            cols = slice(m0, m0 + width)
-            nc.vector.quantize_mx(out=x_codes[a][:, cols].bitcast(FP8X4), scales=x_scales[a][:, cols], in_=grouped[:])
+        def interleaved(tile):
+            return tile.rearrange("p (c i t) -> p c t i", i=RUN, t=PACK)
 
-        def table_pass(dst, g, t, a, cols, start, stop):
-            nc.tensor.matmul_mx(
-                out=dst,
-                lhsT=tab_codes[g][:, a, t * P : (t + 1) * P].bitcast(FP4X4),
-                lhsT_scale=tab_planes[a][:, g * K_PASS + t * P : g * K_PASS + (t + 1) * P],
-                rhs=x_codes[a][:, cols].bitcast(FP8X4),
-                rhs_scale=x_scales[a][:, cols],
-                start=start,
-                stop=stop,
+        def by_rows(tile):
+            return tile.rearrange("p t (c i) -> p c t i", i=RUN)
+
+        offsets = keep.tile([P, J // LIST_ROWS], U16, name="offsets")
+        nc.sync.dma_start(offsets[:], offs)
+
+        def load_by_row_tile(queue, vector, name):
+            tile = sbuf([P, GROUPS, PACK], F32, name)
+            queue.dma_start(tile[:], vector.rearrange("(g p t) -> p g t", g=GROUPS, t=PACK))
+            return tile
+
+        cb_sb = load_by_row_tile(nc.sync, cb, "cb_sb")
+
+        scale_window = sbuf([P, T // 4], I32, "scale_window")
+        nc.vector.memset(scale_window[:], 0)
+        scale_rows = tab_scales.bitcast(I32).rearrange("a (q r) w -> r q a w", r=4)
+        for r in range(4):
+            nc.sync.dma_start(scale_window[r:P:SHIFT, :], scale_rows[r])
+
+        word_window = sbuf([P, T], I32, "word_window")
+        nc.sync.dma_start(word_window[:], tab_words[0].rearrange("p t b -> p (t b)").bitcast(I32))
+
+        x_raw = {}
+
+        def load_x(a, c):
+            x_raw[a, c] = sbuf([P, PACK, PIECE], F32, f"x_raw{a}{c}")
+            rows = x[a * PASS : (a + 1) * PASS, c * PIECE : (c + 1) * PIECE]
+            nc.sync.dma_start(x_raw[a, c][:], rows.rearrange("(p t) w -> p t w", t=PACK))
+
+        load_x(0, 0)
+        load_x(1, 0)
+
+        cw_sb = load_by_row_tile(nc.gpsimd, cw, "cw_sb")
+        second_plane = sbuf([P, J // 4], I32, "second_plane")
+        nc.vector.memset(second_plane[96:P, :], 0)
+        al_planes = sbuf([P, GROUPS, N // 4], I32, "al_planes")
+        nc.gpsimd.memset(al_planes[:], 0)
+        for g, scales in enumerate((al8_scales, al4_scales)):
+            for q in range(4):
+                nc.gpsimd.dma_start(al_planes[32 * q : 32 * q + 4, g, :], scales[0, 4 * q : 4 * q + 4, :].bitcast(I32))
+
+        def entries(j0, count):
+            return offsets[:, j0 // LIST_ROWS : (j0 + count) // LIST_ROWS]
+
+        picked_scales = sbuf([P, J], U8, "picked_scales")
+        first_plane = sbuf([P, J // 4], I32, "first_plane")
+        for g in range(GROUPS):
+            nc.vector.tensor_copy(
+                picked_scales[:, g * PASS : (g + 1) * PASS], scale_window[:].bitcast(U8).indirect(entries(g * PASS, PASS))
+            )
+        for g in range(GROUPS):
+            cols = slice(g * PASS, (g + 1) * PASS)
+            nc.vector.tensor_copy(
+                first_plane[:].bitcast(U8)[:, cols].rearrange("p (t c) -> p t c", t=PACK),
+                picked_scales[:, cols].rearrange("p (c t) -> p t c", t=PACK),
+            )
+        load_x(0, 1)
+        nc.sync.dma_start(second_plane[0 : P - SHIFT, :], first_plane[SHIFT:P, :])
+        tab_planes = [first_plane[:].bitcast(U8), second_plane[:].bitcast(U8)]
+        load_x(1, 1)
+        for c in range(2, PIECES):
+            for a in range(PASSES):
+                load_x(a, c)
+        al8_sb = sbuf([P, N], I32, "al8_sb")
+        nc.sync.dma_start(al8_sb[:], al8_words[0].rearrange("p n b -> p (n b)").bitcast(I32))
+        al4_sb = sbuf([P, N // 2], I32, "al4_sb")
+        nc.sync.dma_start(al4_sb[:], al4_words[0].bitcast(I32))
+
+        def pick_words(j0, count, reuse=None):
+            picked = sbuf([P, count], U32, f"picked_words{j0}", reuse)
+            nc.vector.tensor_copy(
+                picked[:].rearrange("p (t c) -> p c t", t=PACK), word_window[:].bitcast(U32).indirect(entries(j0, count))
+            )
+            return picked
+
+        def part_words(codes, picked):
+            nc.vector.tensor_copy(codes, picked[:].bitcast(U16).rearrange("p (t c a) -> p a t c", t=PACK, a=PASSES))
+
+        tab_codes = [sbuf([P, PASSES, PASS], U16, "tab_codes0")]
+        halves = [pick_words(half * PASS // 2, PASS // 2) for half in range(2)]
+        for half in range(2):
+            by_tile = tab_codes[0][:].rearrange("p a (t c) -> p a t c", t=PACK)
+            part_words(by_tile[:, :, :, half * P // 2 : (half + 1) * P // 2], halves[half])
+
+        x_codes = [sbuf([P, M], U32, f"x_codes{a}") for a in range(PASSES)]
+        x_scales = [sbuf([P, M], U8, f"x_scales{a}") for a in range(PASSES)]
+        x_rounded, sums, tanh_out, h_rounded, h_quantised = {}, {}, {}, {}, {}
+
+        def round_x(a, c):
+            x_rounded[a, c] = sbuf([P, PIECE * PACK], BF16, f"x_rounded{a}{c}")
+            split = SCALAR_ROUNDS.get((a, c), 0)
+            for engine, lo, hi in ((nc.scalar, 0, split), (nc.vector, split, PIECE)):
+                if lo < hi:
+                    copy(engine, interleaved(x_rounded[a, c][:, lo * PACK : hi * PACK]), by_rows(x_raw[a, c][:, :, lo:hi]))
+
+        def quantize_x(a, c):
+            cols = slice(c * PIECE, (c + 1) * PIECE)
+            nc.vector.quantize_mx(
+                out=x_codes[a][:, cols].bitcast(FP8X4), scales=x_scales[a][:, cols], in_=x_rounded[a, c][:]
             )
 
-        def narrow_sums(g, m0, width, banks):
-            per_bank = PACK // len(banks)
+        def first_product(g, c, tiles_per_bank):
             for t in range(PACK):
-                if t % per_bank == 0:
-                    d = bank(banks[t // per_bank], f"d{g}_{m0}_{t}")
-                base = (t % per_bank) * width
-                for a in range(2):
-                    for lo in range(0, width, NARROW):
-                        first, last = a == 0 and lo == 0, a == 1 and lo + NARROW == width
-                        table_pass(d[:, base + lo : base + lo + NARROW], g, t, a, slice(m0 + lo, m0 + lo + NARROW), first, last)
-                sums[g, m0, t] = d[:, base : base + width]
+                if t % tiles_per_bank == 0:
+                    bank = next_bank(f"d{g}{c}{t}")
+                sums[g, c, t] = bank[:, t % tiles_per_bank * PIECE : (t % tiles_per_bank + 1) * PIECE]
+                for a in range(PASSES):
+                    for lo in range(0, PIECE, NARROW):
+                        cols = slice(c * PIECE + lo, c * PIECE + lo + NARROW)
+                        nc.tensor.matmul_mx(
+                            out=sums[g, c, t][:, lo : lo + NARROW],
+                            lhsT=tab_codes[g][:, a, t * P : (t + 1) * P].bitcast(FP4X4),
+                            lhsT_scale=tab_planes[a][:, g * PASS + t * P : g * PASS + (t + 1) * P],
+                            rhs=x_codes[a][:, cols].bitcast(FP8X4),
+                            rhs_scale=x_scales[a][:, cols],
+                            start=(a == 0 and lo == 0),
+                            stop=(a == PASSES - 1 and lo + NARROW == PIECE),
+                        )
 
-        def open_wide(g, m0, banks):
-            for t in range(PACK):
-                d = bank(banks[t], f"d{g}_{m0}_{t}")
-                table_pass(d[:], g, t, 0, slice(m0, m0 + BANK), True, False)
-                sums[g, m0, t] = d[:]
+        def prepare_x(c):
+            for a in range(PASSES):
+                round_x(a, c)
+            for a in range(PASSES):
+                quantize_x(a, c)
 
-        def close_wide(g, m0):
-            for t in range(PACK):
-                table_pass(sums[g, m0, t], g, t, 1, slice(m0, m0 + BANK), False, True)
-
-        def wide_sums(g, m0, banks):
-            for t in range(PACK):
-                d = bank(banks[t], f"d{g}_{m0}_{t}")
-                for a in range(2):
-                    table_pass(d[:], g, t, a, slice(m0, m0 + BANK), a == 0, a == 1)
-                sums[g, m0, t] = d[:]
-
-        def tanh(g, m0, lo, width):
-            th = sbuf([P, PACK, width], F32, f"tanh{g}_{m0 + lo}")
+        def tanh(g, c):
+            tanh_out[g, c] = sbuf([P, PACK, PIECE], F32, f"tanh{g}{c}")
             for t in range(PACK):
                 nc.scalar.activation(
-                    out=th[:, t, :], in_=sums[g, m0, t][:, lo : lo + width], func=TANH, bias=cb_sb[:, g, t : t + 1]
+                    out=tanh_out[g, c][:, t, :], in_=sums[g, c, t], func=TANH, bias=cb_sb[:, g, t : t + 1]
                 )
-            for k in range(0, width, NARROW):
-                tanh_out[g, m0 + lo + k] = (th, k)
 
-        def weigh_h(g, m0, width, slot=None):
-            th, lo = tanh_out[g, m0]
-            grouped = sbuf([P, width * PACK], BF16, f"h_grouped{g}_{m0}", slot)
+        def weigh(g, m0, width):
+            c, lo = divmod(m0, PIECE)
+            reuse = "x_raw11" if not h_rounded else None
+            h_rounded[g, m0] = sbuf([P, width * PACK], BF16, f"h_rounded{g}_{m0}", reuse)
+            weights = cw_sb[:, g, :].rearrange("p (c t i) -> p c t i", c=1, i=1)
             nc.vector.tensor_tensor(
-                grouped[:].rearrange("p (c i t) -> p c t i", i=RUN, t=PACK),
-                th[:, :, lo : lo + width].rearrange("p t (c i) -> p c t i", i=RUN),
-                cw_sb[:, g, :].rearrange("p (c t i) -> p c t i", c=1, i=1).to_broadcast([P, width // RUN, PACK, RUN]),
+                interleaved(h_rounded[g, m0][:]),
+                by_rows(tanh_out[g, c][:, :, lo : lo + width]),
+                weights.to_broadcast([P, width // RUN, PACK, RUN]),
                 MULT,
             )
-            h_grouped[g, m0] = (grouped, width)
 
-        def quantize_h(g, m0):
-            grouped, width = h_grouped[g, m0]
-            cols = slice(m0, m0 + width)
-            nc.vector.quantize_mx(out=h_codes[g][:, cols].bitcast(FP8X4), scales=h_scales[g][:, cols], in_=grouped[:])
+        def quantize_h(g, m0, width):
+            codes = sbuf([P, width], U32, f"h_codes{g}_{m0}")
+            scales = sbuf([P, width], U8, f"h_scales{g}_{m0}")
+            nc.vector.quantize_mx(out=codes[:].bitcast(FP8X4), scales=scales[:], in_=h_rounded[g, m0][:])
+            for lo in range(0, width, NARROW):
+                h_quantised[g, m0 + lo] = (codes, scales, lo)
 
-        def output_pass(dst, n, g, cols, start, stop):
+        def output_pass(dst, n, g, m0, width, start, stop):
             if g == 0:
                 weights = al8_sb[:, n * P : (n + 1) * P].bitcast(FP8X4)
             else:
                 weights = al4_sb[:, n * P // 2 : (n + 1) * P // 2].bitcast(FP4X4)
+            codes, scales, lo = h_quantised[g, m0]
             nc.tensor.matmul_mx(
                 out=dst,
                 lhsT=weights,
                 lhsT_scale=al_planes[:, g, :].bitcast(U8)[:, n * P : (n + 1) * P],
-                rhs=h_codes[g][:, cols].bitcast(FP8X4),
-                rhs_scale=h_scales[g][:, cols],
+                rhs=codes[:, lo : lo + width].bitcast(FP8X4),
+                rhs_scale=scales[:, lo : lo + width],
                 start=start,
                 stop=stop,
             )
 
-        def output_sums(m0, width, n0, count, index):
-            y = bank(index, f"y{m0}_{n0}")
-            for i in range(count):
-                base = i * width
-                output_pass(y[:, base : base + width], n0 + i, 0, slice(m0, m0 + width), True, False)
-                step = width if width == BANK else NARROW
-                for lo in range(0, width, step):
-                    output_pass(
-                        y[:, base + lo : base + lo + step], n0 + i, 1, slice(m0 + lo, m0 + lo + step), False, lo + step == width
-                    )
-            y_banks[m0, n0] = (y, width, count)
+        y_banks = {}
 
-        def open_output(m0, width, banks):
-            for n in range(N // P):
-                y = bank(banks[n], f"y{m0}_{n}")
-                output_pass(y[:, :width], n, 0, slice(m0, m0 + width), True, False)
-                y_banks[m0, n] = (y, width, 1)
+        def second_product(c):
+            m0 = c * PIECE
+            for g in range(GROUPS):
+                weigh(g, m0, PIECE)
+            for g in range(GROUPS):
+                quantize_h(g, m0, PIECE)
+            for n0 in range(0, N // P, BANK // PIECE):
+                y_banks[c, n0] = next_bank(f"y{c}{n0}")
+                for i in range(BANK // PIECE):
+                    dst = y_banks[c, n0][:, i * PIECE : (i + 1) * PIECE]
+                    output_pass(dst, n0 + i, 0, m0, PIECE, True, False)
+                    for lo in range(0, PIECE, NARROW):
+                        output_pass(dst[:, lo : lo + NARROW], n0 + i, 1, m0 + lo, NARROW, False, lo + NARROW == PIECE)
 
-        def close_output(m0, n):
-            y, width, count = y_banks[m0, n]
-            output_pass(y[:, :width], n, 1, slice(m0, m0 + width), False, True)
+        def store_rows(staged, n0, m0):
+            count, width = staged.shape[1:]
+            rows = out[n0 * P : (n0 + count) * P, m0 : m0 + width]
+            nc.sync.dma_start(rows.rearrange("(n p) m -> p n m", p=P), staged)
 
-        def store_rows(m0, n0, engines, queue):
-            width = y_banks[m0, n0][1]
-            staged = sbuf([P, len(engines), width], F32, f"y_staged{m0}_{n0}")
-            for i, engine in enumerate(engines):
-                y = y_banks[m0, n0 + i][0]
-                if engine == "v":
-                    nc.vector.tensor_copy(staged[:, i, :], y[:, :width])
-                else:
-                    nc.scalar.copy(staged[:, i, :], y[:, :width])
-            queue.dma_start(
-                out[n0 * P : (n0 + len(engines)) * P, m0 : m0 + width].rearrange("(n p) m -> p n m", p=P), staged[:]
-            )
+        def store(c):
+            for n0 in range(0, N // P, BANK // PIECE):
+                staged = sbuf([P, BANK], F32, f"y_staged{c}{n0}")
+                nc.scalar.copy(staged[:], y_banks[c, n0][:])
+                store_rows(staged[:].rearrange("p (n m) -> p n m", m=PIECE), n0, c * PIECE)
 
-        def store(m0, n0, engine, queue):
-            y, width, count = y_banks[m0, n0]
-            staged = sbuf([P, count * width], F32, f"y_staged{m0}_{n0}")
-            if engine == "v":
-                nc.vector.tensor_copy(staged[:], y[:, : count * width])
-            else:
-                nc.scalar.copy(staged[:], y[:, : count * width])
-            queue.dma_start(
-                out[n0 * P : (n0 + count) * P, m0 : m0 + width].rearrange("(n p) m -> p n m", p=P),
-                staged[:].rearrange("p (n m) -> p n m", n=count),
-            )
-
-        nc.sync.dma_start(offsets[:], offs)
-        load_vector(nc.sync, cb_sb, cb)
-        load_scale_rows(nc.sync)
-        load_words()
-        load_x(0, 0, 256)
-        load_x(1, 0, 256)
-        load_vector(nc.gpsimd, cw_sb, cw)
-        warm_up()
-        nc.vector.memset(shifted[96:P, :], 0)
-        nc.gpsimd.memset(al_planes[:], 0)
-        load_al_scales(nc.gpsimd)
-        pick_scales(0, 512)
-        pick_scales(512, 512)
-        order_scales(0, 1)
-        order_scales(1, 2)
-        load_x(0, 256, 256)
-        shift_scales(nc.sync, 0, 2)
-        load_x(1, 256, 256)
-        load_x(0, 512, 256)
-        load_x(1, 512, 256)
-        load_x(0, 768, 256)
-        load_x(1, 768, 256)
-        load_al(nc.sync)
-        pick_words(0, 0)
-        pick_words(0, 1)
-        part_words(0, 0)
-        part_words(0, 1)
-        round_x(0, 0, 256, "s")
-        round_x(1, 0, 256, "s")
+        for a in range(PASSES):
+            round_x(a, 0)
         quantize_x(0, 0)
-        pick_words(1, 0, "x_raw0_0")
+        picked = pick_words(PASS, PASS, "x_raw00")
         quantize_x(1, 0)
-        pick_words(1, 1, "x_raw1_0")
-        narrow_sums(0, 0, 256, (0, 1, 2, 3))
-        round_x(0, 256, 256, "s")
-        part_words(1, 0)
-        part_words(1, 1)
-        tanh(0, 0, 0, 256)
-        round_x(1, 256, 256, "v")
-        narrow_sums(1, 0, 256, (4, 5))
-        quantize_x(0, 256)
-        quantize_x(1, 256)
-        narrow_sums(0, 256, 256, (6, 7))
-        narrow_sums(1, 256, 256, (0, 1))
-        round_x(0, 512, 256, "s")
-        tanh(1, 0, 0, 256)
-        weigh_h(0, 0, 256)
-        round_x(1, 512, 256, "v")
-        tanh(0, 256, 0, 256)
-        quantize_x(0, 512)
-        quantize_x(1, 512)
-        narrow_sums(0, 512, 256, (2, 3))
-        narrow_sums(1, 512, 256, (4, 5))
-        tanh(1, 256, 0, 256)
-        weigh_h(1, 0, 256)
-        quantize_h(0, 0)
-        round_x(0, 768, 256, "v")
-        quantize_h(1, 0)
-        round_x(1, 768, 256, "v")
-        output_sums(0, 256, 0, 2, 6)
-        output_sums(0, 256, 2, 2, 7)
-        tanh(0, 512, 0, 256)
-        quantize_x(0, 768)
-        quantize_x(1, 768)
-        narrow_sums(0, 768, 256, (0, 1))
-        narrow_sums(1, 768, 256, (2, 3))
-        weigh_h(0, 256, 256)
-        weigh_h(1, 256, 256)
-        tanh(1, 512, 0, 256)
-        store(0, 0, "s", nc.sync)
-        store(0, 2, "s", nc.sync)
-        quantize_h(0, 256)
-        quantize_h(1, 256)
-        output_sums(256, 256, 0, 2, 4)
-        output_sums(256, 256, 2, 2, 5)
-        tanh(0, 768, 0, 256)
-        weigh_h(0, 512, 256)
-        weigh_h(1, 512, 256)
-        tanh(1, 768, 0, 256)
-        store(256, 0, "s", nc.sync)
-        store(256, 2, "s", nc.sync)
-        quantize_h(0, 512)
-        quantize_h(1, 512)
-        output_sums(512, 256, 0, 2, 6)
-        output_sums(512, 256, 2, 2, 7)
-        weigh_h(0, 768, 256)
-        weigh_h(1, 768, 128)
-        store(512, 0, "s", nc.sync)
-        store(512, 2, "s", nc.sync)
-        quantize_h(0, 768)
-        open_output(768, 128, (0, 1, 2, 3))
-        quantize_h(1, 768)
-        for n in range(4):
-            close_output(768, n)
-        open_output(896, 128, (4, 5, 6, 7))
-        weigh_h(1, 896, 128)
-        quantize_h(1, 896)
-        store_rows(768, 0, "ss", nc.sync)
-        store_rows(768, 2, "ss", nc.sync)
-        for n in range(4):
-            close_output(896, n)
-        store_rows(896, 0, "vs", nc.sync)
-        store_rows(896, 2, "vs", nc.sync)
+        tab_codes.append(sbuf([P, PASSES, PASS], U16, "tab_codes1", "x_raw10"))
+        part_words(tab_codes[1][:].rearrange("p a (t c) -> p a t c", t=PACK), picked)
+        first_product(0, 0, 1)
+        first_product(1, 0, BANK // PIECE)
+
+        for c in range(PIECES):
+            if c + 1 < PIECES:
+                prepare_x(c + 1)
+            for g in range(GROUPS):
+                tanh(g, c)
+                if c + 1 < PIECES:
+                    first_product(g, c + 1, BANK // PIECE)
+            if c >= 1:
+                second_product(c - 1)
+            if c >= 2:
+                store(c - 2)
+
+        last = (PIECES - 1) * PIECE
+        tiles = range(N // P)
+
+        def open_half(m0):
+            banks = [next_bank(f"y_half{m0}_{n}") for n in tiles]
+            for n in tiles:
+                output_pass(banks[n][:, :NARROW], n, 0, m0, NARROW, True, False)
+            return banks
+
+        def close_half(banks, m0):
+            for n in tiles:
+                output_pass(banks[n][:, :NARROW], n, 1, m0, NARROW, False, True)
+
+        def store_half(banks, m0, engines):
+            for n0 in range(0, N // P, len(engines)):
+                staged = sbuf([P, len(engines), NARROW], F32, f"y_half_staged{m0}_{n0}")
+                for i, engine in enumerate(engines):
+                    copy(engine, staged[:, i, :], banks[n0 + i][:, :NARROW])
+                store_rows(staged[:], n0, m0)
+
+        weigh(0, last, PIECE)
+        weigh(1, last, NARROW)
+        store(PIECES - 2)
+        quantize_h(0, last, PIECE)
+        first_half = open_half(last)
+        quantize_h(1, last, NARROW)
+        close_half(first_half, last)
+        second_half = open_half(last + NARROW)
+        weigh(1, last + NARROW, NARROW)
+        quantize_h(1, last + NARROW, NARROW)
+        store_half(first_half, last, (nc.scalar, nc.scalar))
+        close_half(second_half, last + NARROW)
+        store_half(second_half, last + NARROW, (nc.vector, nc.scalar))

@@ -24,13 +24,14 @@ GROUPS = J // PASS
 LIST_ROWS = 16
 BANK = 512
 BANKS = 8
+WORDS_AHEAD = T // 4
 PIECE = 256
 PIECES = M // PIECE
 NARROW = 128
 RUN = 2
 SHIFT = 16
 
-SCALAR_ROUNDS = {(0, 0): PIECE, (1, 0): PIECE, (0, 1): PIECE, (0, 3): PIECE // 2}
+SCALAR_ROUNDS = {(0, 0): PIECE, (1, 0): PIECE, (0, 1): PIECE, (0, 3): PIECE, (1, 3): PIECE // 2}
 
 
 def tile_list_kernl_tanh_mix_none_kernel(
@@ -73,14 +74,17 @@ def tile_list_kernl_tanh_mix_none_kernel(
 
         cb_sb = load_by_row_tile(nc.sync, cb, "cb_sb")
 
+        word_window = sbuf([P, T], I32, "word_window")
+        words = tab_words[0].rearrange("p t b -> p (t b)").bitcast(I32)
+        nc.sync.dma_start(word_window[:, :WORDS_AHEAD], words[:, :WORDS_AHEAD])
+
         scale_window = sbuf([P, T // 4], I32, "scale_window")
         nc.vector.memset(scale_window[:], 0)
         scale_rows = tab_scales.bitcast(I32).rearrange("a (q r) w -> r q a w", r=4)
         for r in range(4):
             nc.sync.dma_start(scale_window[r:P:SHIFT, :], scale_rows[r])
 
-        word_window = sbuf([P, T], I32, "word_window")
-        nc.sync.dma_start(word_window[:], tab_words[0].rearrange("p t b -> p (t b)").bitcast(I32))
+        nc.sync.dma_start(word_window[:, WORDS_AHEAD:], words[:, WORDS_AHEAD:])
 
         x_raw = {}
 

@@ -24,14 +24,13 @@ GROUPS = J // PASS
 LIST_ROWS = 16
 BANK = 512
 BANKS = 8
-WORDS_AHEAD = T // 4
 PIECE = 256
 PIECES = M // PIECE
 NARROW = 128
 RUN = 2
 SHIFT = 16
 
-SCALAR_ROUNDS = {(0, 0): PIECE, (1, 0): PIECE, (0, 1): PIECE, (0, 3): PIECE, (1, 3): PIECE // 2}
+SCALAR_ROUNDS = {(1, 0): PIECE, (0, 1): PIECE, (1, 1): PIECE // 2, (0, 3): PIECE, (1, 3): PIECE // 2}
 
 
 def tile_list_kernl_tanh_mix_none_kernel(
@@ -74,9 +73,13 @@ def tile_list_kernl_tanh_mix_none_kernel(
 
         cb_sb = load_by_row_tile(nc.sync, cb, "cb_sb")
 
-        word_window = sbuf([P, T], I32, "word_window")
-        words = tab_words[0].rearrange("p t b -> p (t b)").bitcast(I32)
-        nc.sync.dma_start(word_window[:, :WORDS_AHEAD], words[:, :WORDS_AHEAD])
+        def load_columns(name, a, m0, width):
+            tile = sbuf([P, PACK, width], F32, name)
+            rows = x[a * PASS : (a + 1) * PASS, m0 : m0 + width]
+            nc.sync.dma_start(tile[:], rows.rearrange("(p t) w -> p t w", t=PACK))
+            return tile
+
+        x_early = load_columns("x_early", 0, 0, NARROW)
 
         scale_window = sbuf([P, T // 4], I32, "scale_window")
         nc.vector.memset(scale_window[:], 0)
@@ -84,16 +87,15 @@ def tile_list_kernl_tanh_mix_none_kernel(
         for r in range(4):
             nc.sync.dma_start(scale_window[r:P:SHIFT, :], scale_rows[r])
 
-        nc.sync.dma_start(word_window[:, WORDS_AHEAD:], words[:, WORDS_AHEAD:])
+        word_window = sbuf([P, T], I32, "word_window")
+        nc.sync.dma_start(word_window[:], tab_words[0].rearrange("p t b -> p (t b)").bitcast(I32))
 
         x_raw = {}
 
         def load_x(a, c):
-            x_raw[a, c] = sbuf([P, PACK, PIECE], F32, f"x_raw{a}{c}")
-            rows = x[a * PASS : (a + 1) * PASS, c * PIECE : (c + 1) * PIECE]
-            nc.sync.dma_start(x_raw[a, c][:], rows.rearrange("(p t) w -> p t w", t=PACK))
+            x_raw[a, c] = load_columns(f"x_raw{a}{c}", a, c * PIECE, PIECE)
 
-        load_x(0, 0)
+        x_later = load_columns("x_later", 0, NARROW, PIECE - NARROW)
         load_x(1, 0)
 
         cw_sb = load_by_row_tile(nc.gpsimd, cw, "cw_sb")
@@ -121,9 +123,9 @@ def tile_list_kernl_tanh_mix_none_kernel(
                 picked_scales[:, cols].rearrange("p (c t) -> p t c", t=PACK),
             )
         load_x(0, 1)
+        load_x(1, 1)
         nc.sync.dma_start(second_plane[0 : P - SHIFT, :], first_plane[SHIFT:P, :])
         tab_planes = [first_plane[:].bitcast(U8), second_plane[:].bitcast(U8)]
-        load_x(1, 1)
         for c in range(2, PIECES):
             for a in range(PASSES):
                 load_x(a, c)
@@ -148,9 +150,7 @@ def tile_list_kernl_tanh_mix_none_kernel(
             by_tile = tab_codes[0][:].rearrange("p a (t c) -> p a t c", t=PACK)
             part_words(by_tile[:, :, :, half * P // 2 : (half + 1) * P // 2], halves[half])
 
-        x_codes = [sbuf([P, M], U32, f"x_codes{a}") for a in range(PASSES)]
-        x_scales = [sbuf([P, M], U8, f"x_scales{a}") for a in range(PASSES)]
-        x_rounded, sums, tanh_out, h_rounded, h_quantised = {}, {}, {}, {}, {}
+        x_codes, x_scales, x_rounded, sums, tanh_out, h_rounded, h_quantised = {}, {}, {}, {}, {}, {}, {}
 
         def round_x(a, c):
             x_rounded[a, c] = sbuf([P, PIECE * PACK], BF16, f"x_rounded{a}{c}")
@@ -159,11 +159,10 @@ def tile_list_kernl_tanh_mix_none_kernel(
                 if lo < hi:
                     copy(engine, interleaved(x_rounded[a, c][:, lo * PACK : hi * PACK]), by_rows(x_raw[a, c][:, :, lo:hi]))
 
-        def quantize_x(a, c):
-            cols = slice(c * PIECE, (c + 1) * PIECE)
-            nc.vector.quantize_mx(
-                out=x_codes[a][:, cols].bitcast(FP8X4), scales=x_scales[a][:, cols], in_=x_rounded[a, c][:]
-            )
+        def quantize_x(a, c, reuse=None):
+            x_codes[a, c] = sbuf([P, PIECE], U32, f"x_codes{a}{c}", reuse)
+            x_scales[a, c] = sbuf([P, PIECE], U8, f"x_scales{a}{c}")
+            nc.vector.quantize_mx(out=x_codes[a, c][:].bitcast(FP8X4), scales=x_scales[a, c][:], in_=x_rounded[a, c][:])
 
         def first_product(g, c, tiles_per_bank):
             for t in range(PACK):
@@ -172,13 +171,13 @@ def tile_list_kernl_tanh_mix_none_kernel(
                 sums[g, c, t] = bank[:, t % tiles_per_bank * PIECE : (t % tiles_per_bank + 1) * PIECE]
                 for a in range(PASSES):
                     for lo in range(0, PIECE, NARROW):
-                        cols = slice(c * PIECE + lo, c * PIECE + lo + NARROW)
+                        cols = slice(lo, lo + NARROW)
                         nc.tensor.matmul_mx(
                             out=sums[g, c, t][:, lo : lo + NARROW],
                             lhsT=tab_codes[g][:, a, t * P : (t + 1) * P].bitcast(FP4X4),
                             lhsT_scale=tab_planes[a][:, g * PASS + t * P : g * PASS + (t + 1) * P],
-                            rhs=x_codes[a][:, cols].bitcast(FP8X4),
-                            rhs_scale=x_scales[a][:, cols],
+                            rhs=x_codes[a, c][:, cols].bitcast(FP8X4),
+                            rhs_scale=x_scales[a, c][:, cols],
                             start=(a == 0 and lo == 0),
                             stop=(a == PASSES - 1 and lo + NARROW == PIECE),
                         )
@@ -233,10 +232,12 @@ def tile_list_kernl_tanh_mix_none_kernel(
 
         y_banks = {}
 
+        def weigh_piece(c):
+            for g in range(GROUPS):
+                weigh(g, c * PIECE, PIECE)
+
         def second_product(c):
             m0 = c * PIECE
-            for g in range(GROUPS):
-                weigh(g, m0, PIECE)
             for g in range(GROUPS):
                 quantize_h(g, m0, PIECE)
             for n0 in range(0, N // P, BANK // PIECE):
@@ -258,27 +259,48 @@ def tile_list_kernl_tanh_mix_none_kernel(
                 nc.scalar.copy(staged[:], y_banks[c, n0][:])
                 store_rows(staged[:].rearrange("p (n m) -> p n m", m=PIECE), n0, c * PIECE)
 
-        for a in range(PASSES):
-            round_x(a, 0)
-        quantize_x(0, 0)
-        picked = pick_words(PASS, PASS, "x_raw00")
+        x_codes[0, 0] = sbuf([P, PIECE], U32, "x_codes00")
+        x_scales[0, 0] = sbuf([P, PIECE], U8, "x_scales00")
+        for engine, raw, lo in ((nc.vector, x_early, 0), (nc.scalar, x_later, NARROW)):
+            rounded = sbuf([P, NARROW * PACK], BF16, f"x_rounded_first{lo}")
+            copy(engine, interleaved(rounded[:]), by_rows(raw[:]))
+            cols = slice(lo, lo + NARROW)
+            nc.vector.quantize_mx(out=x_codes[0, 0][:, cols].bitcast(FP8X4), scales=x_scales[0, 0][:, cols], in_=rounded[:])
+        round_x(1, 0)
+        picked = pick_words(PASS, PASS, "x_later")
         quantize_x(1, 0)
         tab_codes.append(sbuf([P, PASSES, PASS], U16, "tab_codes1", "x_raw10"))
         part_words(tab_codes[1][:].rearrange("p a (t c) -> p a t c", t=PACK), picked)
         first_product(0, 0, 1)
         first_product(1, 0, BANK // PIECE)
 
-        for c in range(PIECES):
-            if c + 1 < PIECES:
-                prepare_x(c + 1)
+        def tanh_and_next(c):
             for g in range(GROUPS):
                 tanh(g, c)
-                if c + 1 < PIECES:
-                    first_product(g, c + 1, BANK // PIECE)
-            if c >= 1:
-                second_product(c - 1)
-            if c >= 2:
-                store(c - 2)
+                first_product(g, c + 1, BANK // PIECE)
+
+        prepare_x(1)
+        tanh_and_next(0)
+        prepare_x(2)
+        tanh_and_next(1)
+        weigh_piece(0)
+        second_product(0)
+        for a in range(PASSES):
+            round_x(a, 3)
+        for g in range(GROUPS):
+            tanh(g, 2)
+        weigh_piece(1)
+        quantize_x(0, 3, "tanh01")
+        quantize_x(1, 3, "tanh11")
+        for g in range(GROUPS):
+            first_product(g, 3, BANK // PIECE)
+        second_product(1)
+        store(0)
+        for g in range(GROUPS):
+            tanh(g, 3)
+        weigh_piece(2)
+        second_product(2)
+        store(1)
 
         last = (PIECES - 1) * PIECE
         tiles = range(N // P)

@@ -30,7 +30,7 @@ NARROW = 128
 RUN = 2
 SHIFT = 16
 
-SCALAR_ROUNDS = {(1, 0): PIECE, (0, 1): PIECE, (1, 1): PIECE // 2, (0, 3): PIECE, (1, 3): PIECE // 2}
+SCALAR_ROUNDS = {(0, 0): PIECE, (1, 0): PIECE, (0, 1): PIECE, (0, 2): PIECE, (0, 3): PIECE}
 
 
 def tile_list_kernl_tanh_mix_none_kernel(
@@ -79,7 +79,9 @@ def tile_list_kernl_tanh_mix_none_kernel(
             nc.sync.dma_start(tile[:], rows.rearrange("(p t) w -> p t w", t=PACK))
             return tile
 
-        x_early = load_columns("x_early", 0, 0, NARROW)
+        word_window = sbuf([P, T], I32, "word_window")
+        words = tab_words[0].rearrange("p t b -> p (t b)").bitcast(I32)
+        nc.sync.dma_start(word_window[:, : T // 4], words[:, : T // 4])
 
         scale_window = sbuf([P, T // 4], I32, "scale_window")
         nc.vector.memset(scale_window[:], 0)
@@ -87,15 +89,14 @@ def tile_list_kernl_tanh_mix_none_kernel(
         for r in range(4):
             nc.sync.dma_start(scale_window[r:P:SHIFT, :], scale_rows[r])
 
-        word_window = sbuf([P, T], I32, "word_window")
-        nc.sync.dma_start(word_window[:], tab_words[0].rearrange("p t b -> p (t b)").bitcast(I32))
+        nc.sync.dma_start(word_window[:, T // 4 :], words[:, T // 4 :])
 
         x_raw = {}
 
         def load_x(a, c):
             x_raw[a, c] = load_columns(f"x_raw{a}{c}", a, c * PIECE, PIECE)
 
-        x_later = load_columns("x_later", 0, NARROW, PIECE - NARROW)
+        load_x(0, 0)
         load_x(1, 0)
 
         cw_sb = load_by_row_tile(nc.gpsimd, cw, "cw_sb")
@@ -123,32 +124,28 @@ def tile_list_kernl_tanh_mix_none_kernel(
                 picked_scales[:, cols].rearrange("p (c t) -> p t c", t=PACK),
             )
         load_x(0, 1)
-        load_x(1, 1)
         nc.sync.dma_start(second_plane[0 : P - SHIFT, :], first_plane[SHIFT:P, :])
         tab_planes = [first_plane[:].bitcast(U8), second_plane[:].bitcast(U8)]
-        for c in range(2, PIECES):
-            for a in range(PASSES):
-                load_x(a, c)
+        load_x(1, 1)
+        load_x(0, 2)
+        load_x(1, 2)
         al8_sb = sbuf([P, N], I32, "al8_sb")
         nc.sync.dma_start(al8_sb[:], al8_words[0].rearrange("p n b -> p (n b)").bitcast(I32))
         al4_sb = sbuf([P, N // 2], I32, "al4_sb")
         nc.sync.dma_start(al4_sb[:], al4_words[0].bitcast(I32))
+        load_x(0, 3)
+        load_x(1, 3)
 
         def pick_words(j0, count, reuse=None):
             picked = sbuf([P, count], U32, f"picked_words{j0}", reuse)
-            nc.vector.tensor_copy(
-                picked[:].rearrange("p (t c) -> p c t", t=PACK), word_window[:].bitcast(U32).indirect(entries(j0, count))
-            )
+            nc.vector.tensor_copy(picked[:], word_window[:].bitcast(U32).indirect(entries(j0, count)))
             return picked
 
         def part_words(codes, picked):
-            nc.vector.tensor_copy(codes, picked[:].bitcast(U16).rearrange("p (t c a) -> p a t c", t=PACK, a=PASSES))
-
-        tab_codes = [sbuf([P, PASSES, PASS], U16, "tab_codes0")]
-        halves = [pick_words(half * PASS // 2, PASS // 2) for half in range(2)]
-        for half in range(2):
-            by_tile = tab_codes[0][:].rearrange("p a (t c) -> p a t c", t=PACK)
-            part_words(by_tile[:, :, :, half * P // 2 : (half + 1) * P // 2], halves[half])
+            nc.vector.tensor_copy(
+                codes.rearrange("p a t (c i) -> p a c t i", i=RUN),
+                picked[:].bitcast(U16).rearrange("p (c i t a) -> p a c t i", i=RUN, t=PACK, a=PASSES),
+            )
 
         x_codes, x_scales, x_rounded, sums, tanh_out, h_rounded, h_quantised = {}, {}, {}, {}, {}, {}, {}
 
@@ -169,7 +166,8 @@ def tile_list_kernl_tanh_mix_none_kernel(
                 if t % tiles_per_bank == 0:
                     bank = next_bank(f"d{g}{c}{t}")
                 sums[g, c, t] = bank[:, t % tiles_per_bank * PIECE : (t % tiles_per_bank + 1) * PIECE]
-                for a in range(PASSES):
+                order = range(PASSES) if (g, c) == (0, 0) else range(PASSES - 1, -1, -1)
+                for a in order:
                     for lo in range(0, PIECE, NARROW):
                         cols = slice(lo, lo + NARROW)
                         nc.tensor.matmul_mx(
@@ -178,34 +176,31 @@ def tile_list_kernl_tanh_mix_none_kernel(
                             lhsT_scale=tab_planes[a][:, g * PASS + t * P : g * PASS + (t + 1) * P],
                             rhs=x_codes[a, c][:, cols].bitcast(FP8X4),
                             rhs_scale=x_scales[a, c][:, cols],
-                            start=(a == 0 and lo == 0),
-                            stop=(a == PASSES - 1 and lo + NARROW == PIECE),
+                            start=(a == order[0] and lo == 0),
+                            stop=(a == order[-1] and lo + NARROW == PIECE),
                         )
 
-        def prepare_x(c):
-            for a in range(PASSES):
-                round_x(a, c)
-            for a in range(PASSES):
-                quantize_x(a, c)
-
-        def tanh(g, c):
-            tanh_out[g, c] = sbuf([P, PACK, PIECE], F32, f"tanh{g}{c}")
+        def tanh(g, c, lo=0, width=PIECE):
+            tanh_out[g, c * PIECE + lo] = sbuf([P, PACK, width], F32, f"tanh{g}{c}_{lo}")
             for t in range(PACK):
                 nc.scalar.activation(
-                    out=tanh_out[g, c][:, t, :], in_=sums[g, c, t], func=TANH, bias=cb_sb[:, g, t : t + 1]
+                    out=tanh_out[g, c * PIECE + lo][:, t, :],
+                    in_=sums[g, c, t][:, lo : lo + width],
+                    func=TANH,
+                    bias=cb_sb[:, g, t : t + 1],
                 )
 
-        def weigh(g, m0, width):
-            c, lo = divmod(m0, PIECE)
+        def weigh(g, m0, width, lo=0):
             reuse = "x_raw11" if not h_rounded else None
-            h_rounded[g, m0] = sbuf([P, width * PACK], BF16, f"h_rounded{g}_{m0}", reuse)
+            h_rounded[g, m0] = sbuf([P, width * PACK], BF16, f"h_rounded{g}_{m0 + lo}", reuse)
             weights = cw_sb[:, g, :].rearrange("p (c t i) -> p c t i", c=1, i=1)
             nc.vector.tensor_tensor(
                 interleaved(h_rounded[g, m0][:]),
-                by_rows(tanh_out[g, c][:, :, lo : lo + width]),
+                by_rows(tanh_out[g, m0][:, :, lo : lo + width]),
                 weights.to_broadcast([P, width // RUN, PACK, RUN]),
                 MULT,
             )
+            return h_rounded[g, m0]
 
         def quantize_h(g, m0, width):
             codes = sbuf([P, width], U32, f"h_codes{g}_{m0}")
@@ -232,14 +227,8 @@ def tile_list_kernl_tanh_mix_none_kernel(
 
         y_banks = {}
 
-        def weigh_piece(c):
-            for g in range(GROUPS):
-                weigh(g, c * PIECE, PIECE)
-
         def second_product(c):
             m0 = c * PIECE
-            for g in range(GROUPS):
-                quantize_h(g, m0, PIECE)
             for n0 in range(0, N // P, BANK // PIECE):
                 y_banks[c, n0] = next_bank(f"y{c}{n0}")
                 for i in range(BANK // PIECE):
@@ -259,49 +248,54 @@ def tile_list_kernl_tanh_mix_none_kernel(
                 nc.scalar.copy(staged[:], y_banks[c, n0][:])
                 store_rows(staged[:].rearrange("p (n m) -> p n m", m=PIECE), n0, c * PIECE)
 
-        x_codes[0, 0] = sbuf([P, PIECE], U32, "x_codes00")
-        x_scales[0, 0] = sbuf([P, PIECE], U8, "x_scales00")
-        for engine, raw, lo in ((nc.vector, x_early, 0), (nc.scalar, x_later, NARROW)):
-            rounded = sbuf([P, NARROW * PACK], BF16, f"x_rounded_first{lo}")
-            copy(engine, interleaved(rounded[:]), by_rows(raw[:]))
-            cols = slice(lo, lo + NARROW)
-            nc.vector.quantize_mx(out=x_codes[0, 0][:, cols].bitcast(FP8X4), scales=x_scales[0, 0][:, cols], in_=rounded[:])
-        round_x(1, 0)
-        picked = pick_words(PASS, PASS, "x_later")
-        quantize_x(1, 0)
-        tab_codes.append(sbuf([P, PASSES, PASS], U16, "tab_codes1", "x_raw10"))
-        part_words(tab_codes[1][:].rearrange("p a (t c) -> p a t c", t=PACK), picked)
-        first_product(0, 0, 1)
-        first_product(1, 0, BANK // PIECE)
+        pairs = BANK // PIECE
+        def part_half(codes, picked, half):
+            by_tile = codes[:].rearrange("p a (t c) -> p a t c", t=PACK)
+            part_words(by_tile[:, :, :, half * P // 2 : (half + 1) * P // 2], picked)
 
-        def tanh_and_next(c):
-            for g in range(GROUPS):
-                tanh(g, c)
-                first_product(g, c + 1, BANK // PIECE)
-
-        prepare_x(1)
-        tanh_and_next(0)
-        prepare_x(2)
-        tanh_and_next(1)
-        weigh_piece(0)
-        second_product(0)
+        tab_codes = [sbuf([P, PASSES, PASS], U16, "tab_codes0")]
+        halves = [pick_words(half * PASS // 2, PASS // 2) for half in range(2)]
+        for half in range(2):
+            part_half(tab_codes[0], halves[half], half)
+        halves = []
         for a in range(PASSES):
-            round_x(a, 3)
-        for g in range(GROUPS):
-            tanh(g, 2)
-        weigh_piece(1)
-        quantize_x(0, 3, "tanh01")
-        quantize_x(1, 3, "tanh11")
-        for g in range(GROUPS):
-            first_product(g, 3, BANK // PIECE)
-        second_product(1)
-        store(0)
-        for g in range(GROUPS):
-            tanh(g, 3)
-        weigh_piece(2)
-        second_product(2)
-        store(1)
+            round_x(a, 0)
+            quantize_x(a, 0)
+            halves.append(pick_words(PASS + a * PASS // 2, PASS // 2, f"x_raw{a}0"))
+        tab_codes.append(sbuf([P, PASSES, PASS], U16, "tab_codes1", "x_rounded10"))
+        for half in range(2):
+            part_half(tab_codes[1], halves[half], half)
+        first_product(0, 0, 1)
+        first_product(1, 0, 1)
+        round_x(0, 1)
+        quantize_x(0, 1)
+        round_x(1, 1)
+        quantize_x(1, 1)
+        first_product(0, 1, pairs)
+        tanh(0, 0)
+        first_product(1, 1, pairs)
 
+        for c in range(PIECES - 1):
+            tanh(1, c)
+            ahead = c + 2 < PIECES
+            if ahead:
+                round_x(0, c + 2)
+            for g in range(GROUPS):
+                weigh(g, c * PIECE, PIECE)
+            if ahead:
+                round_x(1, c + 2)
+            for i in range(2):
+                if ahead:
+                    quantize_x(i, c + 2)
+                quantize_h(i, c * PIECE, PIECE)
+            tanh(0, c + 1)
+            if c > 0:
+                store(c - 1)
+            if ahead:
+                first_product(0, c + 2, pairs)
+            second_product(c)
+            if ahead:
+                first_product(1, c + 2, pairs)
         last = (PIECES - 1) * PIECE
         tiles = range(N // P)
 
@@ -315,6 +309,15 @@ def tile_list_kernl_tanh_mix_none_kernel(
             for n in tiles:
                 output_pass(banks[n][:, :NARROW], n, 1, m0, NARROW, False, True)
 
+        def finish_in_quarters(m0):
+            codes = sbuf([P, NARROW], U32, "h_codes_last")
+            scales = sbuf([P, NARROW], U8, "h_scales_last")
+            parts = [slice(lo, lo + NARROW // 2) for lo in range(0, NARROW, NARROW // 2)]
+            rounded = [weigh(1, m0, NARROW // 2, cols.start) for cols in parts]
+            for cols, values in zip(parts, rounded):
+                nc.vector.quantize_mx(out=codes[:, cols].bitcast(FP8X4), scales=scales[:, cols], in_=values[:])
+            h_quantised[1, m0] = (codes, scales, 0)
+
         def store_half(banks, m0, engines):
             for n0 in range(0, N // P, len(engines)):
                 staged = sbuf([P, len(engines), NARROW], F32, f"y_half_staged{m0}_{n0}")
@@ -322,6 +325,9 @@ def tile_list_kernl_tanh_mix_none_kernel(
                     copy(engine, staged[:, i, :], banks[n0 + i][:, :NARROW])
                 store_rows(staged[:], n0, m0)
 
+        c = PIECES - 1
+        tanh(1, c, 0, NARROW)
+        tanh(1, c, NARROW, NARROW)
         weigh(0, last, PIECE)
         weigh(1, last, NARROW)
         store(PIECES - 2)
@@ -330,8 +336,7 @@ def tile_list_kernl_tanh_mix_none_kernel(
         quantize_h(1, last, NARROW)
         close_half(first_half, last)
         second_half = open_half(last + NARROW)
-        weigh(1, last + NARROW, NARROW)
-        quantize_h(1, last + NARROW, NARROW)
+        finish_in_quarters(last + NARROW)
         store_half(first_half, last, (nc.scalar, nc.scalar))
         close_half(second_half, last + NARROW)
         store_half(second_half, last + NARROW, (nc.vector, nc.scalar))

@@ -30,7 +30,7 @@ NARROW = 128
 RUN = 2
 SHIFT = 16
 
-SCALAR_ROUNDS = {(0, 0): PIECE, (1, 0): PIECE, (0, 1): PIECE, (0, 2): PIECE, (0, 3): PIECE}
+SCALAR_ROUNDS = {(0, 0): PIECE, (1, 0): PIECE, (0, 1): PIECE, (0, 2): PIECE, (0, 3): PIECE // 2}
 
 
 def tile_list_kernl_tanh_mix_none_kernel(
@@ -71,7 +71,6 @@ def tile_list_kernl_tanh_mix_none_kernel(
             queue.dma_start(tile[:], vector.rearrange("(g p t) -> p g t", g=GROUPS, t=PACK))
             return tile
 
-        cb_sb = load_by_row_tile(nc.sync, cb, "cb_sb")
 
         def load_columns(name, a, m0, width):
             tile = sbuf([P, PACK, width], F32, name)
@@ -126,15 +125,15 @@ def tile_list_kernl_tanh_mix_none_kernel(
         load_x(0, 1)
         nc.sync.dma_start(second_plane[0 : P - SHIFT, :], first_plane[SHIFT:P, :])
         tab_planes = [first_plane[:].bitcast(U8), second_plane[:].bitcast(U8)]
+        cb_sb = load_by_row_tile(nc.sync, cb, "cb_sb")
         load_x(1, 1)
-        load_x(0, 2)
-        load_x(1, 2)
+        for c in range(2, PIECES):
+            for a in range(PASSES):
+                load_x(a, c)
         al8_sb = sbuf([P, N], I32, "al8_sb")
         nc.sync.dma_start(al8_sb[:], al8_words[0].rearrange("p n b -> p (n b)").bitcast(I32))
         al4_sb = sbuf([P, N // 2], I32, "al4_sb")
         nc.sync.dma_start(al4_sb[:], al4_words[0].bitcast(I32))
-        load_x(0, 3)
-        load_x(1, 3)
 
         def pick_words(j0, count, reuse=None):
             picked = sbuf([P, count], U32, f"picked_words{j0}", reuse)
@@ -280,14 +279,14 @@ def tile_list_kernl_tanh_mix_none_kernel(
             ahead = c + 2 < PIECES
             if ahead:
                 round_x(0, c + 2)
-            for g in range(GROUPS):
-                weigh(g, c * PIECE, PIECE)
+            weigh(0, c * PIECE, PIECE)
             if ahead:
                 round_x(1, c + 2)
-            for i in range(2):
-                if ahead:
-                    quantize_x(i, c + 2)
-                quantize_h(i, c * PIECE, PIECE)
+                for a in range(PASSES):
+                    quantize_x(a, c + 2)
+            weigh(1, c * PIECE, PIECE)
+            for g in range(GROUPS):
+                quantize_h(g, c * PIECE, PIECE)
             tanh(0, c + 1)
             if c > 0:
                 store(c - 1)

@@ -30,7 +30,7 @@ NARROW = 128
 RUN = 2
 SHIFT = 16
 
-SCALAR_ROUNDS = {(0, 0): PIECE, (1, 0): PIECE, (0, 1): PIECE, (0, 2): PIECE, (0, 3): PIECE // 2}
+SCALAR_ROUNDS = {(0, 0): PIECE, (1, 0): PIECE, (0, 1): PIECE, (0, 2): PIECE // 2, (0, 3): PIECE}
 
 
 def tile_list_kernl_tanh_mix_none_kernel(
@@ -98,6 +98,7 @@ def tile_list_kernl_tanh_mix_none_kernel(
         load_x(0, 0)
         load_x(1, 0)
 
+        cb_sb = load_by_row_tile(nc.gpsimd, cb, "cb_sb")
         cw_sb = load_by_row_tile(nc.gpsimd, cw, "cw_sb")
         second_plane = sbuf([P, J // 4], I32, "second_plane")
         nc.vector.memset(second_plane[96:P, :], 0)
@@ -125,7 +126,6 @@ def tile_list_kernl_tanh_mix_none_kernel(
         load_x(0, 1)
         nc.sync.dma_start(second_plane[0 : P - SHIFT, :], first_plane[SHIFT:P, :])
         tab_planes = [first_plane[:].bitcast(U8), second_plane[:].bitcast(U8)]
-        cb_sb = load_by_row_tile(nc.sync, cb, "cb_sb")
         load_x(1, 1)
         for c in range(2, PIECES):
             for a in range(PASSES):
@@ -256,20 +256,25 @@ def tile_list_kernl_tanh_mix_none_kernel(
         halves = [pick_words(half * PASS // 2, PASS // 2) for half in range(2)]
         for half in range(2):
             part_half(tab_codes[0], halves[half], half)
-        halves = []
-        for a in range(PASSES):
-            round_x(a, 0)
-            quantize_x(a, 0)
-            halves.append(pick_words(PASS + a * PASS // 2, PASS // 2, f"x_raw{a}0"))
-        tab_codes.append(sbuf([P, PASSES, PASS], U16, "tab_codes1", "x_rounded10"))
-        for half in range(2):
-            part_half(tab_codes[1], halves[half], half)
+        round_x(0, 0)
+        quantize_x(0, 0)
+        round_x(1, 0)
+        picked = pick_words(PASS, PASS, "x_raw00")
+        quantize_x(1, 0)
+        tab_codes.append(sbuf([P, PASSES, PASS], U16, "tab_codes1", "x_raw10"))
+        part_words(tab_codes[1][:].rearrange("p a (t c) -> p a t c", t=PACK), picked)
         first_product(0, 0, 1)
         first_product(1, 0, 1)
         round_x(0, 1)
         quantize_x(0, 1)
-        round_x(1, 1)
-        quantize_x(1, 1)
+        x_codes[1, 1] = sbuf([P, PIECE], U32, "x_codes11")
+        x_scales[1, 1] = sbuf([P, PIECE], U8, "x_scales11")
+        rounded = [sbuf([P, NARROW * PACK], BF16, f"x_rounded11_{lo}") for lo in range(0, PIECE, NARROW)]
+        for half in range(2):
+            nc.vector.tensor_copy(interleaved(rounded[half][:]), by_rows(x_raw[1, 1][:, :, half * NARROW : (half + 1) * NARROW]))
+        for half in range(2):
+            cols = slice(half * NARROW, (half + 1) * NARROW)
+            nc.vector.quantize_mx(out=x_codes[1, 1][:, cols].bitcast(FP8X4), scales=x_scales[1, 1][:, cols], in_=rounded[half][:])
         first_product(0, 1, pairs)
         tanh(0, 0)
         first_product(1, 1, pairs)

@@ -167,17 +167,15 @@ def tile_list_kernl_tanh_mix_none_kernel(
                 sums[g, c, t] = bank[:, t % tiles_per_bank * PIECE : (t % tiles_per_bank + 1) * PIECE]
                 order = range(PASSES) if (g, c) == (0, 0) else range(PASSES - 1, -1, -1)
                 for a in order:
-                    for lo in range(0, PIECE, NARROW):
-                        cols = slice(lo, lo + NARROW)
-                        nc.tensor.matmul_mx(
-                            out=sums[g, c, t][:, lo : lo + NARROW],
-                            lhsT=tab_codes[g][:, a, t * P : (t + 1) * P].bitcast(FP4X4),
-                            lhsT_scale=tab_planes[a][:, g * PASS + t * P : g * PASS + (t + 1) * P],
-                            rhs=x_codes[a, c][:, cols].bitcast(FP8X4),
-                            rhs_scale=x_scales[a, c][:, cols],
-                            start=(a == order[0] and lo == 0),
-                            stop=(a == order[-1] and lo + NARROW == PIECE),
-                        )
+                    nc.tensor.matmul_mx(
+                        out=sums[g, c, t],
+                        lhsT=tab_codes[g][:, a, t * P : (t + 1) * P].bitcast(FP4X4),
+                        lhsT_scale=tab_planes[a][:, g * PASS + t * P : g * PASS + (t + 1) * P],
+                        rhs=x_codes[a, c][:].bitcast(FP8X4),
+                        rhs_scale=x_scales[a, c][:],
+                        start=(a == order[0]),
+                        stop=(a == order[-1]),
+                    )
 
         def tanh(g, c, lo=0, width=PIECE):
             tanh_out[g, c * PIECE + lo] = sbuf([P, PACK, width], F32, f"tanh{g}{c}_{lo}")
@@ -233,8 +231,7 @@ def tile_list_kernl_tanh_mix_none_kernel(
                 for i in range(BANK // PIECE):
                     dst = y_banks[c, n0][:, i * PIECE : (i + 1) * PIECE]
                     output_pass(dst, n0 + i, 0, m0, PIECE, True, False)
-                    for lo in range(0, PIECE, NARROW):
-                        output_pass(dst[:, lo : lo + NARROW], n0 + i, 1, m0 + lo, NARROW, False, lo + NARROW == PIECE)
+                    output_pass(dst, n0 + i, 1, m0, PIECE, False, True)
 
         def store_rows(staged, n0, m0):
             count, width = staged.shape[1:]

@@ -67,8 +67,8 @@ def tile_list_kernl_tanh_mix_none_kernel(
         nc.sync.dma_start(offsets[:], offs)
 
         def load_by_row_tile(queue, vector, name):
-            tile = sbuf([P, GROUPS, PACK], F32, name)
-            queue.dma_start(tile[:], vector.rearrange("(g p t) -> p g t", g=GROUPS, t=PACK))
+            tile = sbuf([P, GROUPS, 2 * PACK], F32, name)
+            queue.dma_start(tile[:, :, :PACK], vector.rearrange("(g p t) -> p g t", g=GROUPS, t=PACK))
             return tile
 
 
@@ -98,12 +98,12 @@ def tile_list_kernl_tanh_mix_none_kernel(
         load_x(0, 0)
         load_x(1, 0)
 
-        cb_sb = load_by_row_tile(nc.gpsimd, cb, "cb_sb")
-        cw_sb = load_by_row_tile(nc.gpsimd, cw, "cw_sb")
+        cb_sb = load_by_row_tile(nc.scalar, cb, "cb_sb")
+        cw_sb = load_by_row_tile(nc.scalar, cw, "cw_sb")
         second_plane = sbuf([P, J // 4], I32, "second_plane")
         nc.vector.memset(second_plane[96:P, :], 0)
         al_planes = sbuf([P, GROUPS, N // 4], I32, "al_planes")
-        nc.gpsimd.memset(al_planes[:], 0)
+        nc.vector.memset(al_planes[:], 0)
         for g, scales in enumerate((al8_scales, al4_scales)):
             for q in range(4):
                 nc.gpsimd.dma_start(al_planes[32 * q : 32 * q + 4, g, :], scales[0, 4 * q : 4 * q + 4, :].bitcast(I32))
@@ -190,7 +190,7 @@ def tile_list_kernl_tanh_mix_none_kernel(
         def weigh(g, m0, width, lo=0):
             reuse = "x_raw11" if not h_rounded else None
             h_rounded[g, m0] = sbuf([P, width * PACK], BF16, f"h_rounded{g}_{m0 + lo}", reuse)
-            weights = cw_sb[:, g, :].rearrange("p (c t i) -> p c t i", c=1, i=1)
+            weights = cw_sb[:, g, :PACK].rearrange("p (c t i) -> p c t i", c=1, i=1)
             nc.vector.tensor_tensor(
                 interleaved(h_rounded[g, m0][:]),
                 by_rows(tanh_out[g, m0][:, :, lo : lo + width]),

from contextlib import ExitStack

import concourse.mybir as mybir

K, M, N, J, T = 1024, 1024, 512, 1024, 2048
FLOPS = 2 * K * J * M + 2 * J * N * M

F32 = mybir.dt.float32
BF16 = mybir.dt.bfloat16
I32 = mybir.dt.int32
U32 = mybir.dt.uint32
U16 = mybir.dt.uint16
U8 = mybir.dt.uint8
FP8X4 = mybir.dt.float8_e4m3fn_x4
FP4X4 = mybir.dt.float4_e2m1fn_x4
TANH = mybir.ActivationFunctionType.Tanh
MULT = mybir.AluOpType.mult

P = 128
PACK = 4
PASS = P * PACK
PASSES = K // PASS
GROUPS = J // PASS
LIST_ROWS = 16
BANK = 512
BANKS = 8
PIECE = 256
PIECES = M // PIECE
NARROW = 128
RUN = 2
SHIFT = 16

SCALAR_ROUNDS = {(0, 0): PIECE, (1, 0): PIECE, (0, 1): PIECE, (0, 2): PIECE // 2, (0, 3): PIECE}


def tile_list_kernl_tanh_mix_none_kernel(
    tc, x, tab_words, tab_scales, cw, cb, al8_words, al8_scales, al4_words, al4_scales, offs, out
):
    nc = tc.nc
    with ExitStack() as ctx:
        keep = ctx.enter_context(tc.tile_pool(name="keep", bufs=1))
        share = ctx.enter_context(tc.tile_pool(name="share", bufs=1))
        psum = ctx.enter_context(tc.psum_pool(name="psum", bufs=1))

        def sbuf(shape, dtype, name, reuse=None):
            return share.tile(shape, dtype, name=name, tag=reuse or name, align_bytes=64)

        handed_out = []

        def next_bank(name):
            handed_out.append(name)
            return psum.tile([P, BANK], F32, name=name, tag=f"bank{(len(handed_out) - 1) % BANKS}")

        def copy(engine, dst, src):
            if engine is nc.vector:
                nc.vector.tensor_copy(dst, src)
            else:
                nc.scalar.copy(dst, src)

        def interleaved(tile):
            return tile.rearrange("p (c i t) -> p c t i", i=RUN, t=PACK)

        def by_rows(tile):
            return tile.rearrange("p t (c i) -> p c t i", i=RUN)

        offsets = keep.tile([P, J // LIST_ROWS], U16, name="offsets")
        nc.sync.dma_start(offsets[:], offs)

        def load_by_row_tile(queue, vector, name):
            tile = sbuf([P, GROUPS, 2 * PACK], F32, name)
            queue.dma_start(tile[:, :, :PACK], vector.rearrange("(g p t) -> p g t", g=GROUPS, t=PACK))
            return tile


        def load_columns(name, a, m0, width):
            tile = sbuf([P, PACK, width], F32, name)
            rows = x[a * PASS : (a + 1) * PASS, m0 : m0 + width]
            nc.sync.dma_start(tile[:], rows.rearrange("(p t) w -> p t w", t=PACK))
            return tile

        word_window = sbuf([P, T], I32, "word_window")
        words = tab_words[0].rearrange("p t b -> p (t b)").bitcast(I32)
        nc.sync.dma_start(word_window[:, : T // 4], words[:, : T // 4])

        scale_window = sbuf([P, T // 4], I32, "scale_window")
        nc.vector.memset(scale_window[:], 0)
        scale_rows = tab_scales.bitcast(I32).rearrange("a (q r) w -> r q a w", r=4)
        for r in range(4):
            nc.sync.dma_start(scale_window[r:P:SHIFT, :], scale_rows[r])

        nc.sync.dma_start(word_window[:, T // 4 :], words[:, T // 4 :])

        x_raw = {}

        def load_x(a, c):
            x_raw[a, c] = load_columns(f"x_raw{a}{c}", a, c * PIECE, PIECE)

        load_x(0, 0)
        load_x(1, 0)

        cb_sb = load_by_row_tile(nc.scalar, cb, "cb_sb")
        cw_sb = load_by_row_tile(nc.scalar, cw, "cw_sb")
        second_plane = sbuf([P, J // 4], I32, "second_plane")
        nc.vector.memset(second_plane[96:P, :], 0)
        al_planes = sbuf([P, GROUPS, N // 4], I32, "al_planes")
        nc.vector.memset(al_planes[:], 0)
        for g, scales in enumerate((al8_scales, al4_scales)):
            for q in range(4):
                nc.gpsimd.dma_start(al_planes[32 * q : 32 * q + 4, g, :], scales[0, 4 * q : 4 * q + 4, :].bitcast(I32))

        def entries(j0, count):
            return offsets[:, j0 // LIST_ROWS : (j0 + count) // LIST_ROWS]

        picked_scales = sbuf([P, J], U8, "picked_scales")
        first_plane = sbuf([P, J // 4], I32, "first_plane")
        for g in range(GROUPS):
            nc.vector.tensor_copy(
                picked_scales[:, g * PASS : (g + 1) * PASS], scale_window[:].bitcast(U8).indirect(entries(g * PASS, PASS))
            )
        for g in range(GROUPS):
            cols = slice(g * PASS, (g + 1) * PASS)
            nc.vector.tensor_copy(
                first_plane[:].bitcast(U8)[:, cols].rearrange("p (t c) -> p t c", t=PACK),
                picked_scales[:, cols].rearrange("p (c t) -> p t c", t=PACK),
            )
        load_x(0, 1)
        nc.sync.dma_start(second_plane[0 : P - SHIFT, :], first_plane[SHIFT:P, :])
        tab_planes = [first_plane[:].bitcast(U8), second_plane[:].bitcast(U8)]
        load_x(1, 1)
        for c in range(2, PIECES):
            for a in range(PASSES):
                load_x(a, c)
        al8_sb = sbuf([P, N], I32, "al8_sb")
        nc.sync.dma_start(al8_sb[:], al8_words[0].rearrange("p n b -> p (n b)").bitcast(I32))
        al4_sb = sbuf([P, N // 2], I32, "al4_sb")
        nc.sync.dma_start(al4_sb[:], al4_words[0].bitcast(I32))

        def pick_words(j0, count, reuse=None):
            picked = sbuf([P, count], U32, f"picked_words{j0}", reuse)
            nc.vector.tensor_copy(picked[:], word_window[:].bitcast(U32).indirect(entries(j0, count)))
            return picked

        def part_words(codes, picked):
            nc.vector.tensor_copy(
                codes.rearrange("p a t (c i) -> p a c t i", i=RUN),
                picked[:].bitcast(U16).rearrange("p (c i t a) -> p a c t i", i=RUN, t=PACK, a=PASSES),
            )

        x_codes, x_scales, x_rounded, sums, tanh_out, h_rounded, h_quantised = {}, {}, {}, {}, {}, {}, {}

        def round_x(a, c):
            x_rounded[a, c] = sbuf([P, PIECE * PACK], BF16, f"x_rounded{a}{c}")
            split = SCALAR_ROUNDS.get((a, c), 0)
            for engine, lo, hi in ((nc.scalar, 0, split), (nc.vector, split, PIECE)):
                if lo < hi:
                    copy(engine, interleaved(x_rounded[a, c][:, lo * PACK : hi * PACK]), by_rows(x_raw[a, c][:, :, lo:hi]))

        def quantize_x(a, c, reuse=None):
            x_codes[a, c] = sbuf([P, PIECE], U32, f"x_codes{a}{c}", reuse)
            x_scales[a, c] = sbuf([P, PIECE], U8, f"x_scales{a}{c}")
            nc.vector.quantize_mx(out=x_codes[a, c][:].bitcast(FP8X4), scales=x_scales[a, c][:], in_=x_rounded[a, c][:])

        def first_product(g, c, tiles_per_bank):
            for t in range(PACK):
                if t % tiles_per_bank == 0:
                    bank = next_bank(f"d{g}{c}{t}")
                sums[g, c, t] = bank[:, t % tiles_per_bank * PIECE : (t % tiles_per_bank + 1) * PIECE]
                order = range(PASSES) if (g, c) == (0, 0) else range(PASSES - 1, -1, -1)
                for a in order:
                    nc.tensor.matmul_mx(
                        out=sums[g, c, t],
                        lhsT=tab_codes[g][:, a, t * P : (t + 1) * P].bitcast(FP4X4),
                        lhsT_scale=tab_planes[a][:, g * PASS + t * P : g * PASS + (t + 1) * P],
                        rhs=x_codes[a, c][:].bitcast(FP8X4),
                        rhs_scale=x_scales[a, c][:],
                        start=(a == order[0]),
                        stop=(a == order[-1]),
                    )

        def tanh(g, c, lo=0, width=PIECE):
            tanh_out[g, c * PIECE + lo] = sbuf([P, PACK, width], F32, f"tanh{g}{c}_{lo}")
            for t in range(PACK):
                nc.scalar.activation(
                    out=tanh_out[g, c * PIECE + lo][:, t, :],
                    in_=sums[g, c, t][:, lo : lo + width],
                    func=TANH,
                    bias=cb_sb[:, g, t : t + 1],
                )

        def weigh(g, m0, width, lo=0):
            reuse = "x_raw11" if not h_rounded else None
            h_rounded[g, m0] = sbuf([P, width * PACK], BF16, f"h_rounded{g}_{m0 + lo}", reuse)
            weights = cw_sb[:, g, :PACK].rearrange("p (c t i) -> p c t i", c=1, i=1)
            nc.vector.tensor_tensor(
                interleaved(h_rounded[g, m0][:]),
                by_rows(tanh_out[g, m0][:, :, lo : lo + width]),
                weights.to_broadcast([P, width // RUN, PACK, RUN]),
                MULT,
            )
            return h_rounded[g, m0]

        def quantize_h(g, m0, width):
            codes = sbuf([P, width], U32, f"h_codes{g}_{m0}")
            scales = sbuf([P, width], U8, f"h_scales{g}_{m0}")
            nc.vector.quantize_mx(out=codes[:].bitcast(FP8X4), scales=scales[:], in_=h_rounded[g, m0][:])
            for lo in range(0, width, NARROW):
                h_quantised[g, m0 + lo] = (codes, scales, lo)

        def output_pass(dst, n, g, m0, width, start, stop):
            if g == 0:
                weights = al8_sb[:, n * P : (n + 1) * P].bitcast(FP8X4)
            else:
                weights = al4_sb[:, n * P // 2 : (n + 1) * P // 2].bitcast(FP4X4)
            codes, scales, lo = h_quantised[g, m0]
            nc.tensor.matmul_mx(
                out=dst,
                lhsT=weights,
                lhsT_scale=al_planes[:, g, :].bitcast(U8)[:, n * P : (n + 1) * P],
                rhs=codes[:, lo : lo + width].bitcast(FP8X4),
                rhs_scale=scales[:, lo : lo + width],
                start=start,
                stop=stop,
            )

        y_banks = {}

        def second_product(c):
            m0 = c * PIECE
            for n0 in range(0, N // P, BANK // PIECE):
                y_banks[c, n0] = next_bank(f"y{c}{n0}")
                for i in range(BANK // PIECE):
                    dst = y_banks[c, n0][:, i * PIECE : (i + 1) * PIECE]
                    output_pass(dst, n0 + i, 0, m0, PIECE, True, False)
                    output_pass(dst, n0 + i, 1, m0, PIECE, False, True)

        def store_rows(staged, n0, m0):
            count, width = staged.shape[1:]
            rows = out[n0 * P : (n0 + count) * P, m0 : m0 + width]
            nc.sync.dma_start(rows.rearrange("(n p) m -> p n m", p=P), staged)

        def store(c):
            for n0 in range(0, N // P, BANK // PIECE):
                staged = sbuf([P, BANK], F32, f"y_staged{c}{n0}")
                nc.scalar.copy(staged[:], y_banks[c, n0][:])
                store_rows(staged[:].rearrange("p (n m) -> p n m", m=PIECE), n0, c * PIECE)

        pairs = BANK // PIECE
        def part_half(codes, picked, half):
            by_tile = codes[:].rearrange("p a (t c) -> p a t c", t=PACK)
            part_words(by_tile[:, :, :, half * P // 2 : (half + 1) * P // 2], picked)

        tab_codes = [sbuf([P, PASSES, PASS], U16, "tab_codes0")]
        halves = [pick_words(half * PASS // 2, PASS // 2) for half in range(2)]
        for half in range(2):
            part_half(tab_codes[0], halves[half], half)
        round_x(0, 0)
        quantize_x(0, 0)
        round_x(1, 0)
        picked = pick_words(PASS, PASS, "x_raw00")
        quantize_x(1, 0)
        tab_codes.append(sbuf([P, PASSES, PASS], U16, "tab_codes1", "x_raw10"))
        part_words(tab_codes[1][:].rearrange("p a (t c) -> p a t c", t=PACK), picked)
        first_product(0, 0, 1)
        first_product(1, 0, 1)
        round_x(0, 1)
        quantize_x(0, 1)
        x_codes[1, 1] = sbuf([P, PIECE], U32, "x_codes11")
        x_scales[1, 1] = sbuf([P, PIECE], U8, "x_scales11")
        rounded = [sbuf([P, NARROW * PACK], BF16, f"x_rounded11_{lo}") for lo in range(0, PIECE, NARROW)]
        for half in range(2):
            nc.vector.tensor_copy(interleaved(rounded[half][:]), by_rows(x_raw[1, 1][:, :, half * NARROW : (half + 1) * NARROW]))
        for half in range(2):
            cols = slice(half * NARROW, (half + 1) * NARROW)
            nc.vector.quantize_mx(out=x_codes[1, 1][:, cols].bitcast(FP8X4), scales=x_scales[1, 1][:, cols], in_=rounded[half][:])
        first_product(0, 1, pairs)
        tanh(0, 0)
        first_product(1, 1, pairs)

        for c in range(PIECES - 1):
            tanh(1, c)
            ahead = c + 2 < PIECES
            if ahead:
                round_x(0, c + 2)
            weigh(0, c * PIECE, PIECE)
            if ahead:
                round_x(1, c + 2)
                for a in range(PASSES):
                    quantize_x(a, c + 2)
            weigh(1, c * PIECE, PIECE)
            for g in range(GROUPS):
                quantize_h(g, c * PIECE, PIECE)
            tanh(0, c + 1)
            if c > 0:
                store(c - 1)
            if ahead:
                first_product(0, c + 2, pairs)
            second_product(c)
            if ahead:
                first_product(1, c + 2, pairs)
        last = (PIECES - 1) * PIECE
        tiles = range(N // P)

        def open_half(m0):
            banks = [next_bank(f"y_half{m0}_{n}") for n in tiles]
            for n in tiles:
                output_pass(banks[n][:, :NARROW], n, 0, m0, NARROW, True, False)
            return banks

        def close_half(banks, m0):
            for n in tiles:
                output_pass(banks[n][:, :NARROW], n, 1, m0, NARROW, False, True)

        def finish_in_quarters(m0):
            codes = sbuf([P, NARROW], U32, "h_codes_last")
            scales = sbuf([P, NARROW], U8, "h_scales_last")
            parts = [slice(lo, lo + NARROW // 2) for lo in range(0, NARROW, NARROW // 2)]
            rounded = [weigh(1, m0, NARROW // 2, cols.start) for cols in parts]
            for cols, values in zip(parts, rounded):
                nc.vector.quantize_mx(out=codes[:, cols].bitcast(FP8X4), scales=scales[:, cols], in_=values[:])
            h_quantised[1, m0] = (codes, scales, 0)

        def store_half(banks, m0, engines):
            for n0 in range(0, N // P, len(engines)):
                staged = sbuf([P, len(engines), NARROW], F32, f"y_half_staged{m0}_{n0}")
                for i, engine in enumerate(engines):
                    copy(engine, staged[:, i, :], banks[n0 + i][:, :NARROW])
                store_rows(staged[:], n0, m0)

        c = PIECES - 1
        tanh(1, c, 0, NARROW)
        tanh(1, c, NARROW, NARROW)
        weigh(0, last, PIECE)
        weigh(1, last, NARROW)
        store(PIECES - 2)
        quantize_h(0, last, PIECE)
        first_half = open_half(last)
        quantize_h(1, last, NARROW)
        close_half(first_half, last)
        second_half = open_half(last + NARROW)
        finish_in_quarters(last + NARROW)
        store_half(first_half, last, (nc.scalar, nc.scalar))
        close_half(second_half, last + NARROW)
        store_half(second_half, last + NARROW, (nc.vector, nc.scalar))
